import numpy as np
import ml_dtypes


def mxq(x, axis, fmt="e4m3"):
    dtype, down = {"e4m3": (ml_dtypes.float8_e4m3fn, 7), "e5m2": (ml_dtypes.float8_e5m2, 14)}[fmt]
    v = np.moveaxis(np.asarray(x, np.float32).astype(ml_dtypes.bfloat16).astype(np.float64), axis, -1)
    blocks = v.reshape(v.shape[:-1] + (-1, 32))
    amax = np.abs(blocks).max(-1, keepdims=True)
    byte = np.maximum(np.where(amax > 0, np.frexp(amax)[1] - 1 + 127, 0) - down, 1)
    scale = np.exp2(byte - 127.0)
    codes = (blocks / scale).astype(np.float32).astype(dtype).astype(np.float64)
    return np.moveaxis((codes * scale).reshape(v.shape), -1, axis)


WIDE = False


def mx_kscale(k):
    if not WIDE:
        return np.ones(k)
    levels = np.array([10, -10, 5, -5, 0])
    if k % 512:
        return np.exp2(np.random.permutation(np.resize(levels, k // 32))).repeat(32)
    a = np.empty((k // 512, 16))
    for p in range(k // 512):
        a[p, :8] = np.random.permutation(np.resize(levels, 8))
        for g in range(8):
            far = levels[np.abs(levels - a[p, g]) >= 10]
            a[p, g + 8] = far[np.random.randint(len(far))]
    return np.exp2(a.ravel()).repeat(32)


def f64(x):
    return np.asarray(x).astype(np.float64)


def striped(idx):
    return np.tile(idx.reshape(-1, 16).T, (8, 1)).astype(np.uint16)


def unstriped(offs):
    return offs[:16].T.reshape(-1).astype(np.int64)


def striped8(idx):
    return np.concatenate([x.reshape(-1, 16).T for x in idx]).astype(np.uint16)


def runs(offs, k):
    lists = np.stack([offs[16 * r : 16 * r + 16].T.reshape(-1) for r in range(8)]).astype(np.int64)
    return lists[np.arange(k) % 512 // 64]


def pack_weight(w):
    k, n = w.shape
    w = f64(np.asarray(w, np.float32).astype(ml_dtypes.bfloat16)).reshape(k // 32, 32, n)
    amax = np.abs(w).max(1)
    byte = np.clip(np.where(amax > 0, np.frexp(amax)[1] - 1 + 127 - 7, 1), 1, 254)
    scaled = (w * np.exp2(127.0 - byte)[:, None, :]).reshape(k, n).astype(np.float32)
    words = np.ascontiguousarray(scaled.reshape(k // 512, 128, 4, n).transpose(0, 1, 3, 2)).astype(ml_dtypes.float8_e4m3fn).view(np.uint8)
    return words, np.ascontiguousarray(byte.astype(np.uint8).reshape(k // 512, 16, n))


def unpack_weight(words, scales):
    g, p, n, _ = words.shape
    vals = np.ascontiguousarray(words).view(ml_dtypes.float8_e4m3fn).astype(np.float64) * np.repeat(np.exp2(scales.astype(np.float64) - 127.0), 8, axis=1)[..., None]
    return vals.transpose(0, 1, 3, 2).reshape(g * 512, n)


def sigmoid(v):
    return 1.0 / (1.0 + np.exp(-np.maximum(v, -700.0)))

def planes(y):
    n, m = y.shape
    v = y.astype(np.float32).astype(ml_dtypes.bfloat16).astype(np.float64).reshape(n // 32, 32, m)
    top = np.abs(v).max(1)
    byte = np.clip(np.where(top > 0, np.frexp(top)[1] - 1 + 127 - 7, 1), 1, 254)
    codes = (v * np.exp2(127.0 - byte)[:, None, :]).reshape(n, m).astype(np.float32).astype(ml_dtypes.float8_e4m3fn).view(np.uint8)
    words = codes.reshape(n // 512, 128, 4, m).transpose(0, 1, 3, 2)
    return np.ascontiguousarray(words), np.ascontiguousarray(byte.astype(np.uint8).reshape(n // 512, 16, m))


K, T, S, N = 512, 2048, 512, 512


def setup_inputs():
    n = np.random.standard_normal
    s = mx_kscale(K)[:, None]
    packed_xT = pack_weight(n((K, T)) * s)
    return {
        "x_words": packed_xT[0],
        "x_scales": packed_xT[1],
        "w1": (n((K, N)) / np.sqrt(K) / s).astype(np.float32),
        "w2": (n((K, N)) / np.sqrt(K) / s).astype(np.float32),
        "offs": striped8(np.stack([np.random.permutation(T)[:S] for _ in range(8)])),
        "own": striped(np.random.permutation(T)[:S]),
    }


def reference(x_words, x_scales, w1, w2, offs, own):
    xq = unpack_weight(x_words, x_scales)[np.arange(K)[:, None], runs(offs, K)]
    y = mxq(f64(w1), 0, "e4m3").T @ xq
    xown = unpack_weight(x_words, x_scales)[:, unstriped(own)]
    e = mxq(f64(w2), 0, "e4m3").T @ xown
    out_0 = sigmoid(y) * e
    return (out_0,) + planes(out_0)

@@ -1,0 +1,165 @@
+from contextlib import ExitStack
+
+import concourse.mybir as mybir
+
+K, T, S, N = 512, 2048, 512, 512
+FLOPS = 2 * 2 * K * N * S
+
+F32 = mybir.dt.float32
+BF16 = mybir.dt.bfloat16
+I32 = mybir.dt.int32
+U32 = mybir.dt.uint32
+U16 = mybir.dt.uint16
+U8 = mybir.dt.uint8
+FP8X4 = mybir.dt.float8_e4m3fn_x4
+SIGMOID = mybir.ActivationFunctionType.Sigmoid
+MULT = mybir.AluOpType.mult
+
+P = 128
+PACK = 4
+QUAD = 32
+BLOCK_P = 8
+HALF = N // 2
+HALF_P = HALF // PACK
+UNITS = [(0, 256, 0, 2), (0, 256, 2, 2), (256, 128, 0, 4), (384, 128, 0, 4)]
+
+
+def tile_picked_phmix_sigmoid_po_kernel(
+    tc, x_words, x_scales, w1, w2, offs, own, out_0, out_1, out_2
+):
+    nc = tc.nc
+    with ExitStack() as ctx:
+        lists = ctx.enter_context(tc.tile_pool(name="lists", bufs=1))
+        reuse = ctx.enter_context(tc.tile_pool(name="reuse", bufs=1))
+        keep = ctx.enter_context(tc.tile_pool(name="keep", bufs=1))
+        psum = ctx.enter_context(tc.psum_pool(name="psum", bufs=1))
+
+        byte_table = reuse.tile([P, T], U8, name="byte_table", offset=0, align_bytes=64)
+        nc.vector.memset(byte_table[:].bitcast(I32), 0)
+
+        offs_sb = lists.tile([P, S // 16], U16, name="offs_sb")
+        own_sb = lists.tile([P, S // 16], U16, name="own_sb")
+        nc.sync.dma_start(offs_sb[:], offs)
+        nc.sync.dma_start(own_sb[:], own)
+        nc.sync.dma_start(byte_table[0:P:BLOCK_P, :].bitcast(I32), x_scales[0].bitcast(I32))
+
+        word_table = reuse.tile([P, T], I32, name="word_table", offset=4096, align_bytes=64)
+        nc.scalar.dma_start(word_table[:], x_words[0].rearrange("p c r -> p (c r)").bitcast(I32))
+        raw = {}
+        for name, w in (("w1", w1), ("w2", w2)):
+            rows = w.rearrange("(p j) c -> p j c", j=PACK)
+            for h in range(2):
+                raw[name, h] = keep.tile([P, PACK, HALF], F32, name=f"raw_{name}_{h}", align_bytes=64)
+                nc.scalar.dma_start(raw[name, h][:], rows[:, :, h * HALF : (h + 1) * HALF])
+
+        x_planes = keep.tile([P, 2 * S], U8, name="x_planes", align_bytes=64)
+        nc.vector.memset(x_planes[:].bitcast(I32), 0)
+
+        warm = keep.tile([P, 8], F32, name="warm")
+        nc.vector.memset(warm[:], 0.0)
+        warm_out = keep.tile([P, 8], F32, name="warm_out")
+        nc.scalar.activation(warm_out[:], warm[:], SIGMOID)
+
+        picked_bytes = keep.tile([P, 2 * S], U8, name="picked_bytes", align_bytes=64)
+        nc.vector.tensor_copy(picked_bytes[:, 0:S], byte_table[:].indirect(offs_sb[:]))
+        nc.vector.tensor_copy(picked_bytes[:, S : 2 * S], byte_table[:].indirect(own_sb[:]))
+        for q in range(P // QUAD):
+            nc.sync.dma_start(
+                x_planes[QUAD * q : QUAD * q + 4, :].bitcast(I32),
+                picked_bytes[QUAD * q : QUAD * (q + 1) : BLOCK_P, :].bitcast(I32),
+            )
+
+        picked_words = reuse.tile([P, 2 * S], U32, name="picked_words", offset=0, align_bytes=64)
+        nc.vector.tensor_copy(picked_words[:, 0:S], word_table[:].bitcast(U32).indirect(offs_sb[:]))
+        nc.vector.tensor_copy(picked_words[:, S : 2 * S], word_table[:].bitcast(U32).indirect(own_sb[:]))
+
+        def deal(copy, name, h, offset):
+            dealt = reuse.tile([P, PACK, HALF_P, PACK], BF16, name=f"dealt_{name}_{h}", offset=offset, align_bytes=64)
+            copy(
+                dealt[:].rearrange("p t m j -> p m j t"),
+                raw[name, h][:].rearrange("p j (m t) -> p m j t", t=PACK),
+            )
+            return dealt
+
+        def quantise(codes, scales, dealt, h):
+            for t in range(PACK):
+                cols = slice(t * P + h * HALF_P, t * P + (h + 1) * HALF_P)
+                nc.vector.quantize_mx(
+                    out=codes[:, cols].bitcast(FP8X4),
+                    scales=scales[:, cols],
+                    in_=dealt[:, t, :, :].rearrange("p m j -> p (m j)"),
+                )
+
+        def product(codes, scales, first, name, u):
+            c0, width, t0, nt = UNITS[u]
+            acc = psum.tile([P, nt, width], F32, name=f"{name}_{u}")
+            for i in range(nt):
+                cols = slice((t0 + i) * P, (t0 + i + 1) * P)
+                nc.tensor.matmul_mx(
+                    out=acc[:, i, :],
+                    lhsT=codes[:, cols].bitcast(FP8X4),
+                    lhsT_scale=scales[:, cols],
+                    rhs=picked_words[:, first + c0 : first + c0 + width].bitcast(FP8X4),
+                    rhs_scale=x_planes[:, first + c0 : first + c0 + width],
+                    start=True,
+                    stop=True,
+                )
+            return acc
+
+        w1_codes = reuse.tile([P, N], U32, name="w1_codes", offset=10240, align_bytes=64)
+        w1_scales = keep.tile([P, N], U8, name="w1_scales", align_bytes=64)
+        w2_codes = keep.tile([P, N], U32, name="w2_codes", align_bytes=64)
+        w2_scales = keep.tile([P, N], U8, name="w2_scales", align_bytes=64)
+
+        w1_dealt = [deal(nc.scalar.copy, "w1", 0, 12288), deal(nc.vector.tensor_copy, "w1", 1, 4096)]
+        quantise(w1_codes, w1_scales, w1_dealt[0], 0)
+        quantise(w1_codes, w1_scales, w1_dealt[1], 1)
+
+        gates = []
+        for u, (c0, width, t0, nt) in enumerate(UNITS):
+            acc = product(w1_codes, w1_scales, 0, "y", u)
+            gate = keep.tile([P, nt, width], F32, name=f"gate_{u}", align_bytes=64)
+            nc.scalar.activation(gate[:], acc[:], SIGMOID)
+            gates.append(gate)
+
+        for h in range(2):
+            dealt = deal(nc.vector.tensor_copy, "w2", h, 6144 + 2048 * h)
+            quantise(w2_codes, w2_scales, dealt, h)
+
+        out_rows = out_0.rearrange("(p t) c -> p t c", t=PACK)
+        out_words = out_1[0].rearrange("p c r -> p (c r)").bitcast(I32)
+        codes = keep.tile([P, S], I32, name="codes", align_bytes=64)
+        scales = keep.tile([P, S], U8, name="scales", align_bytes=64)
+        results = {}
+        for c0, width in ((0, 256), (256, 128), (384, 128)):
+            results[c0] = keep.tile([P, PACK, width], F32, name=f"result_{c0}", align_bytes=64)
+
+        def finish(copy, c0, width):
+            rounded = keep.tile([P, width, PACK], BF16, name=f"rounded_{c0}", align_bytes=64)
+            copy(
+                rounded[:].rearrange("p (c i) t -> p c t i", i=4),
+                results[c0][:].rearrange("p t (c i) -> p c t i", i=4),
+            )
+            nc.vector.quantize_mx(
+                out=codes[:, c0 : c0 + width].bitcast(FP8X4),
+                scales=scales[:, c0 : c0 + width],
+                in_=rounded[:].rearrange("p c t -> p (c t)"),
+            )
+
+        for u, (c0, width, t0, nt) in enumerate(UNITS):
+            acc = product(w2_codes, w2_scales, S, "e", u)
+            part = results[c0][:, t0 : t0 + nt, :]
+            nc.vector.tensor_tensor(part, acc[:], gates[u][:], MULT)
+            nc.sync.dma_start(out_rows[:, t0 : t0 + nt, c0 : c0 + width], part)
+
+        finish(nc.scalar.copy, 0, 256)
+        nc.sync.dma_start(out_words[:, 0:256], codes[:, 0:256])
+        finish(nc.scalar.copy, 256, 128)
+        finish(nc.vector.tensor_copy, 384, 128)
+        nc.sync.dma_start(out_words[:, 256:512], codes[:, 256:512])
+        for q in range(P // QUAD):
+            queue = nc.scalar if q % 2 else nc.sync
+            queue.dma_start(
+                out_2[0, 4 * q : 4 * q + 4, :].bitcast(I32),
+                scales[QUAD * q : QUAD * q + 4, :].bitcast(I32),
+            )

@@ -21,7 +21,8 @@ QUAD = 32
 BLOCK_P = 8
 HALF = N // 2
 HALF_P = HALF // PACK
-UNITS = [(0, 256, 0, 2), (0, 256, 2, 2), (256, 128, 0, 4), (384, 128, 0, 4)]
+PAIRS = (slice(0, 2), slice(2, 4))
+PLACES = S // 2
 
 
 def tile_picked_phmix_sigmoid_po_kernel(
@@ -30,35 +31,30 @@ def tile_picked_phmix_sigmoid_po_kernel(
     nc = tc.nc
     with ExitStack() as ctx:
         lists = ctx.enter_context(tc.tile_pool(name="lists", bufs=1))
-        reuse = ctx.enter_context(tc.tile_pool(name="reuse", bufs=1))
         keep = ctx.enter_context(tc.tile_pool(name="keep", bufs=1))
         psum = ctx.enter_context(tc.psum_pool(name="psum", bufs=1))
-
-        byte_table = reuse.tile([P, T], U8, name="byte_table", offset=0, align_bytes=64)
-        nc.vector.memset(byte_table[:].bitcast(I32), 0)
 
         offs_sb = lists.tile([P, S // 16], U16, name="offs_sb")
         own_sb = lists.tile([P, S // 16], U16, name="own_sb")
         nc.sync.dma_start(offs_sb[:], offs)
         nc.sync.dma_start(own_sb[:], own)
-        nc.sync.dma_start(byte_table[0:P:BLOCK_P, :].bitcast(I32), x_scales[0].bitcast(I32))
 
-        word_table = reuse.tile([P, T], I32, name="word_table", offset=4096, align_bytes=64)
-        nc.scalar.dma_start(word_table[:], x_words[0].rearrange("p c r -> p (c r)").bitcast(I32))
-        raw = {}
-        for name, w in (("w1", w1), ("w2", w2)):
-            rows = w.rearrange("(p j) c -> p j c", j=PACK)
-            for h in range(2):
-                raw[name, h] = keep.tile([P, PACK, HALF], F32, name=f"raw_{name}_{h}", align_bytes=64)
-                nc.scalar.dma_start(raw[name, h][:], rows[:, :, h * HALF : (h + 1) * HALF])
+        byte_table = keep.tile([P, T], U8, name="byte_table", tag="bytes_then_w2", align_bytes=64)
+        scale_rows = x_scales[0].bitcast(I32).unsqueeze(1).to_broadcast([P // BLOCK_P, BLOCK_P, T // 4])
+        nc.sync.dma_start(byte_table[:].bitcast(I32), scale_rows)
+        word_table = keep.tile([P, T], I32, name="word_table", align_bytes=64)
+        nc.sync.dma_start(word_table[:], x_words[0].rearrange("p c r -> p (c r)").bitcast(I32))
+
+        def load_half(w, h, tag):
+            raw = keep.tile([P, PACK, HALF], F32, name=tag, tag=tag, align_bytes=64)
+            nc.sync.dma_start(raw[:], w.rearrange("(p j) c -> p j c", j=PACK)[:, :, h * HALF : (h + 1) * HALF])
+            return raw
+
+        w1_raw = [load_half(w1, 0, "w1_left"), load_half(w1, 1, "w1_right")]
+        w2_raw = [load_half(w2, 0, "w2_left")]
 
         x_planes = keep.tile([P, 2 * S], U8, name="x_planes", align_bytes=64)
         nc.vector.memset(x_planes[:].bitcast(I32), 0)
-
-        warm = keep.tile([P, 8], F32, name="warm")
-        nc.vector.memset(warm[:], 0.0)
-        warm_out = keep.tile([P, 8], F32, name="warm_out")
-        nc.scalar.activation(warm_out[:], warm[:], SIGMOID)
 
         picked_bytes = keep.tile([P, 2 * S], U8, name="picked_bytes", align_bytes=64)
         nc.vector.tensor_copy(picked_bytes[:, 0:S], byte_table[:].indirect(offs_sb[:]))
@@ -68,95 +64,98 @@ def tile_picked_phmix_sigmoid_po_kernel(
                 x_planes[QUAD * q : QUAD * q + 4, :].bitcast(I32),
                 picked_bytes[QUAD * q : QUAD * (q + 1) : BLOCK_P, :].bitcast(I32),
             )
+        w2_raw.append(load_half(w2, 1, "bytes_then_w2"))
 
-        picked_words = reuse.tile([P, 2 * S], U32, name="picked_words", offset=0, align_bytes=64)
+        picked_words = keep.tile([P, 2 * S], U32, name="picked_words", align_bytes=64)
         nc.vector.tensor_copy(picked_words[:, 0:S], word_table[:].bitcast(U32).indirect(offs_sb[:]))
         nc.vector.tensor_copy(picked_words[:, S : 2 * S], word_table[:].bitcast(U32).indirect(own_sb[:]))
 
-        def deal(copy, name, h, offset):
-            dealt = reuse.tile([P, PACK, HALF_P, PACK], BF16, name=f"dealt_{name}_{h}", offset=offset, align_bytes=64)
+        def deal(copy, dealt, raw, h, ts):
             copy(
-                dealt[:].rearrange("p t m j -> p m j t"),
-                raw[name, h][:].rearrange("p j (m t) -> p m j t", t=PACK),
+                dealt[:, ts, h * HALF_P : (h + 1) * HALF_P, :].rearrange("p t m j -> p m j t"),
+                raw[:].rearrange("p j (m t) -> p m j t", t=PACK)[:, :, :, ts],
             )
-            return dealt
 
-        def quantise(codes, scales, dealt, h):
-            for t in range(PACK):
-                cols = slice(t * P + h * HALF_P, t * P + (h + 1) * HALF_P)
+        def quantise(name, dealt):
+            codes = keep.tile([P, PACK, P], U32, name=f"{name}_codes", align_bytes=64)
+            scales = keep.tile([P, PACK, P], U8, name=f"{name}_scales", align_bytes=64)
+            for ts in PAIRS:
                 nc.vector.quantize_mx(
-                    out=codes[:, cols].bitcast(FP8X4),
-                    scales=scales[:, cols],
-                    in_=dealt[:, t, :, :].rearrange("p m j -> p (m j)"),
+                    out=codes[:, ts, :].rearrange("p t m -> p (t m)").bitcast(FP8X4),
+                    scales=scales[:, ts, :].rearrange("p t m -> p (t m)"),
+                    in_=dealt[:, ts, :, :].rearrange("p t m j -> p (t m j)"),
                 )
+            return codes, scales
 
-        def product(codes, scales, first, name, u):
-            c0, width, t0, nt = UNITS[u]
-            acc = psum.tile([P, nt, width], F32, name=f"{name}_{u}")
-            for i in range(nt):
-                cols = slice((t0 + i) * P, (t0 + i + 1) * P)
+        def product(name, codes, scales, first, h, ts):
+            acc = psum.tile([P, 2, PLACES], F32, name=f"{name}_{h}_{ts.start}")
+            cols = slice(first + h * PLACES, first + (h + 1) * PLACES)
+            for t in range(ts.start, ts.stop):
                 nc.tensor.matmul_mx(
-                    out=acc[:, i, :],
-                    lhsT=codes[:, cols].bitcast(FP8X4),
-                    lhsT_scale=scales[:, cols],
-                    rhs=picked_words[:, first + c0 : first + c0 + width].bitcast(FP8X4),
-                    rhs_scale=x_planes[:, first + c0 : first + c0 + width],
+                    out=acc[:, t - ts.start, :],
+                    lhsT=codes[:, t, :].bitcast(FP8X4),
+                    lhsT_scale=scales[:, t, :],
+                    rhs=picked_words[:, cols].bitcast(FP8X4),
+                    rhs_scale=x_planes[:, cols],
                     start=True,
                     stop=True,
                 )
             return acc
 
-        w1_codes = reuse.tile([P, N], U32, name="w1_codes", offset=10240, align_bytes=64)
-        w1_scales = keep.tile([P, N], U8, name="w1_scales", align_bytes=64)
-        w2_codes = keep.tile([P, N], U32, name="w2_codes", align_bytes=64)
-        w2_scales = keep.tile([P, N], U8, name="w2_scales", align_bytes=64)
+        w1_dealt = keep.tile([P, PACK, P, PACK], BF16, name="w1_dealt", align_bytes=64)
+        deal(nc.scalar.copy, w1_dealt, w1_raw[0], 0, slice(0, PACK))
+        for ts in PAIRS:
+            deal(nc.vector.tensor_copy, w1_dealt, w1_raw[1], 1, ts)
+        w1_codes, w1_scales = quantise("w1", w1_dealt)
 
-        w1_dealt = [deal(nc.scalar.copy, "w1", 0, 12288), deal(nc.vector.tensor_copy, "w1", 1, 4096)]
-        quantise(w1_codes, w1_scales, w1_dealt[0], 0)
-        quantise(w1_codes, w1_scales, w1_dealt[1], 1)
-
-        gates = []
-        for u, (c0, width, t0, nt) in enumerate(UNITS):
-            acc = product(w1_codes, w1_scales, 0, "y", u)
-            gate = keep.tile([P, nt, width], F32, name=f"gate_{u}", align_bytes=64)
-            nc.scalar.activation(gate[:], acc[:], SIGMOID)
-            gates.append(gate)
-
+        gates = {}
         for h in range(2):
-            dealt = deal(nc.vector.tensor_copy, "w2", h, 6144 + 2048 * h)
-            quantise(w2_codes, w2_scales, dealt, h)
+            for ts in PAIRS:
+                acc = product("y", w1_codes, w1_scales, 0, h, ts)
+                gate = keep.tile([P, 2, PLACES], F32, name=f"gate_{h}_{ts.start}", align_bytes=64)
+                nc.scalar.activation(gate[:], acc[:], SIGMOID)
+                gates[h, ts.start] = gate
+
+        w2_dealt = keep.tile([P, PACK, P, PACK], BF16, name="w2_dealt", align_bytes=64)
+        deal(nc.vector.tensor_copy, w2_dealt, w2_raw[0], 0, slice(0, PACK))
+        for ts in PAIRS:
+            deal(nc.vector.tensor_copy, w2_dealt, w2_raw[1], 1, ts)
+        w2_codes, w2_scales = quantise("w2", w2_dealt)
 
         out_rows = out_0.rearrange("(p t) c -> p t c", t=PACK)
         out_words = out_1[0].rearrange("p c r -> p (c r)").bitcast(I32)
         codes = keep.tile([P, S], I32, name="codes", align_bytes=64)
         scales = keep.tile([P, S], U8, name="scales", align_bytes=64)
-        results = {}
-        for c0, width in ((0, 256), (256, 128), (384, 128)):
-            results[c0] = keep.tile([P, PACK, width], F32, name=f"result_{c0}", align_bytes=64)
 
-        def finish(copy, c0, width):
-            rounded = keep.tile([P, width, PACK], BF16, name=f"rounded_{c0}", align_bytes=64)
+        results = []
+        for h in range(2):
+            result = keep.tile([P, PACK, PLACES], F32, name=f"result_{h}", align_bytes=64)
+            results.append(result)
+            for ts in PAIRS:
+                acc = product("e", w2_codes, w2_scales, S, h, ts)
+                nc.vector.tensor_tensor(result[:, ts, :], acc[:], gates[h, ts.start][:], MULT)
+                nc.sync.dma_start(out_rows[:, ts, h * PLACES : (h + 1) * PLACES], result[:, ts, :])
+
+        def interleave(copy, rounded, result, c0, c1):
             copy(
-                rounded[:].rearrange("p (c i) t -> p c t i", i=4),
-                results[c0][:].rearrange("p t (c i) -> p c t i", i=4),
+                rounded[:, c0:c1, :].rearrange("p (c i) t -> p c t i", i=4),
+                result[:, :, c0:c1].rearrange("p t (c i) -> p c t i", i=4),
             )
+
+        for h in range(2):
+            rounded = keep.tile([P, PLACES, PACK], BF16, name=f"rounded_{h}", align_bytes=64)
+            if h == 0:
+                interleave(nc.scalar.copy, rounded, results[h], 0, PLACES)
+            else:
+                interleave(nc.scalar.copy, rounded, results[h], 0, 96)
+                interleave(nc.vector.tensor_copy, rounded, results[h], 96, PLACES)
+            cols = slice(h * PLACES, (h + 1) * PLACES)
             nc.vector.quantize_mx(
-                out=codes[:, c0 : c0 + width].bitcast(FP8X4),
-                scales=scales[:, c0 : c0 + width],
+                out=codes[:, cols].bitcast(FP8X4),
+                scales=scales[:, cols],
                 in_=rounded[:].rearrange("p c t -> p (c t)"),
             )
-
-        for u, (c0, width, t0, nt) in enumerate(UNITS):
-            acc = product(w2_codes, w2_scales, S, "e", u)
-            part = results[c0][:, t0 : t0 + nt, :]
-            nc.vector.tensor_tensor(part, acc[:], gates[u][:], MULT)
-            nc.sync.dma_start(out_rows[:, t0 : t0 + nt, c0 : c0 + width], part)
-
-        finish(nc.scalar.copy, 0, 256)
-        nc.sync.dma_start(out_words[:, 0:256], codes[:, 0:256])
-        finish(nc.scalar.copy, 256, 128)
-        finish(nc.vector.tensor_copy, 384, 128)
-        nc.sync.dma_start(out_words[:, 256:512], codes[:, 256:512])
+            nc.sync.dma_start(out_words[:, cols], codes[:, cols])
         for q in range(P // QUAD):
             queue = nc.scalar if q % 2 else nc.sync
             queue.dma_start(

@@ -19,10 +19,10 @@ P = 128
 PACK = 4
 QUAD = 32
 BLOCK_P = 8
-HALF = N // 2
-HALF_P = HALF // PACK
+VECTOR_M = 88
 PAIRS = (slice(0, 2), slice(2, 4))
 PLACES = S // 2
+FIRST_UNITS = (slice(0, 1), slice(1, 2), slice(2, 4))
 
 
 def tile_picked_phmix_sigmoid_po_kernel(
@@ -42,19 +42,23 @@ def tile_picked_phmix_sigmoid_po_kernel(
         byte_table = keep.tile([P, T], U8, name="byte_table", tag="bytes_then_w2", align_bytes=64)
         scale_rows = x_scales[0].bitcast(I32).unsqueeze(1).to_broadcast([P // BLOCK_P, BLOCK_P, T // 4])
         nc.sync.dma_start(byte_table[:].bitcast(I32), scale_rows)
-        word_table = keep.tile([P, T], I32, name="word_table", align_bytes=64)
-        nc.sync.dma_start(word_table[:], x_words[0].rearrange("p c r -> p (c r)").bitcast(I32))
 
-        def load_half(w, h, tag):
-            raw = keep.tile([P, PACK, HALF], F32, name=tag, tag=tag, align_bytes=64)
-            nc.sync.dma_start(raw[:], w.rearrange("(p j) c -> p j c", j=PACK)[:, :, h * HALF : (h + 1) * HALF])
+        def load_weight(w, js, tag):
+            raw = keep.tile([P, js.stop - js.start, N], F32, name=f"raw_{tag}", tag=tag, align_bytes=64)
+            nc.sync.dma_start(raw[:], w.rearrange("(p j) c -> p j c", j=PACK)[:, js, :])
             return raw
 
-        w1_raw = [load_half(w1, 0, "w1_left"), load_half(w1, 1, "w1_right")]
-        w2_raw = [load_half(w2, 0, "w2_left")]
+        w1_raw = load_weight(w1, slice(0, PACK), "w1")
+        word_table = keep.tile([P, T], I32, name="word_table", align_bytes=64)
+        nc.sync.dma_start(word_table[:], x_words[0].rearrange("p c r -> p (c r)").bitcast(I32))
+        w2_first = load_weight(w2, PAIRS[0], "w2_then_gate")
 
         x_planes = keep.tile([P, 2 * S], U8, name="x_planes", align_bytes=64)
         nc.vector.memset(x_planes[:].bitcast(I32), 0)
+        warm = keep.tile([P, 8], F32, name="warm")
+        nc.vector.memset(warm[:], 0.0)
+        warm_out = keep.tile([P, 8], F32, name="warm_out")
+        nc.scalar.activation(warm_out[:], warm[:], SIGMOID)
 
         picked_bytes = keep.tile([P, 2 * S], U8, name="picked_bytes", align_bytes=64)
         nc.vector.tensor_copy(picked_bytes[:, 0:S], byte_table[:].indirect(offs_sb[:]))
@@ -64,22 +68,18 @@ def tile_picked_phmix_sigmoid_po_kernel(
                 x_planes[QUAD * q : QUAD * q + 4, :].bitcast(I32),
                 picked_bytes[QUAD * q : QUAD * (q + 1) : BLOCK_P, :].bitcast(I32),
             )
-        w2_raw.append(load_half(w2, 1, "bytes_then_w2"))
+        w2_second = load_weight(w2, PAIRS[1], "bytes_then_w2")
 
-        picked_words = keep.tile([P, 2 * S], U32, name="picked_words", align_bytes=64)
-        nc.vector.tensor_copy(picked_words[:, 0:S], word_table[:].bitcast(U32).indirect(offs_sb[:]))
-        nc.vector.tensor_copy(picked_words[:, S : 2 * S], word_table[:].bitcast(U32).indirect(own_sb[:]))
-
-        def deal(copy, dealt, raw, h, ts):
+        def deal(copy, dealt, raw, js, ms, ts=slice(0, PACK)):
             copy(
-                dealt[:, ts, h * HALF_P : (h + 1) * HALF_P, :].rearrange("p t m j -> p m j t"),
-                raw[:].rearrange("p j (m t) -> p m j t", t=PACK)[:, :, :, ts],
+                dealt[:, ts, ms, js].rearrange("p t m j -> p m j t"),
+                raw[:].rearrange("p j (m t) -> p m j t", t=PACK)[:, ms, :, ts],
             )
 
-        def quantise(name, dealt):
+        def quantise(name, dealt, groups):
             codes = keep.tile([P, PACK, P], U32, name=f"{name}_codes", align_bytes=64)
             scales = keep.tile([P, PACK, P], U8, name=f"{name}_scales", align_bytes=64)
-            for ts in PAIRS:
+            for ts in groups:
                 nc.vector.quantize_mx(
                     out=codes[:, ts, :].rearrange("p t m -> p (t m)").bitcast(FP8X4),
                     scales=scales[:, ts, :].rearrange("p t m -> p (t m)"),
@@ -87,8 +87,8 @@ def tile_picked_phmix_sigmoid_po_kernel(
                 )
             return codes, scales
 
-        def product(name, codes, scales, first, h, ts):
-            acc = psum.tile([P, 2, PLACES], F32, name=f"{name}_{h}_{ts.start}")
+        def product(bank, codes, scales, first, h, ts):
+            acc = psum.tile([P, ts.stop - ts.start, PLACES], F32, name=bank, tag=bank)
             cols = slice(first + h * PLACES, first + (h + 1) * PLACES)
             for t in range(ts.start, ts.stop):
                 nc.tensor.matmul_mx(
@@ -103,24 +103,25 @@ def tile_picked_phmix_sigmoid_po_kernel(
             return acc
 
         w1_dealt = keep.tile([P, PACK, P, PACK], BF16, name="w1_dealt", align_bytes=64)
-        deal(nc.scalar.copy, w1_dealt, w1_raw[0], 0, slice(0, PACK))
-        for ts in PAIRS:
-            deal(nc.vector.tensor_copy, w1_dealt, w1_raw[1], 1, ts)
-        w1_codes, w1_scales = quantise("w1", w1_dealt)
+        deal(nc.scalar.copy, w1_dealt, w1_raw, slice(0, PACK), slice(VECTOR_M, P))
+        deal(nc.vector.tensor_copy, w1_dealt, w1_raw, slice(0, PACK), slice(0, VECTOR_M))
+        w1_codes, w1_scales = quantise("w1", w1_dealt, PAIRS)
 
-        gates = {}
-        for h in range(2):
-            for ts in PAIRS:
-                acc = product("y", w1_codes, w1_scales, 0, h, ts)
-                gate = keep.tile([P, 2, PLACES], F32, name=f"gate_{h}_{ts.start}", align_bytes=64)
-                nc.scalar.activation(gate[:], acc[:], SIGMOID)
-                gates[h, ts.start] = gate
+        picked_words = keep.tile([P, 2 * S], U32, name="picked_words", align_bytes=64)
+        nc.vector.tensor_copy(picked_words[:, 0:S], word_table[:].bitcast(U32).indirect(offs_sb[:]))
+        nc.vector.tensor_copy(picked_words[:, S : 2 * S], word_table[:].bitcast(U32).indirect(own_sb[:]))
 
         w2_dealt = keep.tile([P, PACK, P, PACK], BF16, name="w2_dealt", align_bytes=64)
-        deal(nc.vector.tensor_copy, w2_dealt, w2_raw[0], 0, slice(0, PACK))
+        deal(nc.scalar.copy, w2_dealt, w2_first, PAIRS[0], slice(0, P))
         for ts in PAIRS:
-            deal(nc.vector.tensor_copy, w2_dealt, w2_raw[1], 1, ts)
-        w2_codes, w2_scales = quantise("w2", w2_dealt)
+            deal(nc.vector.tensor_copy, w2_dealt, w2_second, PAIRS[1], slice(0, P), ts)
+        w2_codes, w2_scales = quantise("w2", w2_dealt, FIRST_UNITS)
+
+        gate = keep.tile([P, 2, PACK, PLACES], F32, name="gate", tag="w2_then_gate", align_bytes=64)
+        for h in range(2):
+            for ts in PAIRS:
+                acc = product(f"bank_y_{h}_{ts.start}", w1_codes, w1_scales, 0, h, ts)
+                nc.scalar.activation(gate[:, h, ts, :], acc[:], SIGMOID)
 
         out_rows = out_0.rearrange("(p t) c -> p t c", t=PACK)
         out_words = out_1[0].rearrange("p c r -> p (c r)").bitcast(I32)
@@ -131,9 +132,10 @@ def tile_picked_phmix_sigmoid_po_kernel(
         for h in range(2):
             result = keep.tile([P, PACK, PLACES], F32, name=f"result_{h}", align_bytes=64)
             results.append(result)
-            for ts in PAIRS:
-                acc = product("e", w2_codes, w2_scales, S, h, ts)
-                nc.vector.tensor_tensor(result[:, ts, :], acc[:], gates[h, ts.start][:], MULT)
+            for ts in FIRST_UNITS if h == 0 else PAIRS:
+                bank = "bank_y_0_0" if (h, ts.start) == (1, 2) else f"bank_e_{h}_{ts.start}"
+                acc = product(bank, w2_codes, w2_scales, S, h, ts)
+                nc.vector.tensor_tensor(result[:, ts, :], acc[:], gate[:, h, ts, :], MULT)
                 nc.sync.dma_start(out_rows[:, ts, h * PLACES : (h + 1) * PLACES], result[:, ts, :])
 
         def interleave(copy, rounded, result, c0, c1):

@@ -19,10 +19,10 @@ P = 128
 PACK = 4
 QUAD = 32
 BLOCK_P = 8
-VECTOR_M = 88
 PAIRS = (slice(0, 2), slice(2, 4))
+LEFT, RIGHT = slice(0, P // 2), slice(P // 2, P)
 PLACES = S // 2
-FIRST_UNITS = (slice(0, 1), slice(1, 2), slice(2, 4))
+SCALAR_PLACES = 80
 
 
 def tile_picked_phmix_sigmoid_po_kernel(
@@ -31,6 +31,7 @@ def tile_picked_phmix_sigmoid_po_kernel(
     nc = tc.nc
     with ExitStack() as ctx:
         lists = ctx.enter_context(tc.tile_pool(name="lists", bufs=1))
+        reuse = ctx.enter_context(tc.tile_pool(name="reuse", bufs=1))
         keep = ctx.enter_context(tc.tile_pool(name="keep", bufs=1))
         psum = ctx.enter_context(tc.psum_pool(name="psum", bufs=1))
 
@@ -39,44 +40,54 @@ def tile_picked_phmix_sigmoid_po_kernel(
         nc.sync.dma_start(offs_sb[:], offs)
         nc.sync.dma_start(own_sb[:], own)
 
-        byte_table = keep.tile([P, T], U8, name="byte_table", tag="bytes_then_w2", align_bytes=64)
+        byte_table = reuse.tile([P, T], U8, name="byte_table", offset=3072, align_bytes=64)
         scale_rows = x_scales[0].bitcast(I32).unsqueeze(1).to_broadcast([P // BLOCK_P, BLOCK_P, T // 4])
         nc.sync.dma_start(byte_table[:].bitcast(I32), scale_rows)
 
-        def load_weight(w, js, tag):
-            raw = keep.tile([P, js.stop - js.start, N], F32, name=f"raw_{tag}", tag=tag, align_bytes=64)
-            nc.sync.dma_start(raw[:], w.rearrange("(p j) c -> p j c", j=PACK)[:, js, :])
+        def load_weight(w, ms, name, offset):
+            raw = reuse.tile([P, PACK, PACK * (ms.stop - ms.start)], F32, name=name, offset=offset, align_bytes=64)
+            rows = w.rearrange("(p j) c -> p j c", j=PACK)
+            nc.sync.dma_start(raw[:], rows[:, :, PACK * ms.start : PACK * ms.stop])
             return raw
 
-        w1_raw = load_weight(w1, slice(0, PACK), "w1")
+        w1_raw = load_weight(w1, slice(0, P), "w1_raw", 16384)
         word_table = keep.tile([P, T], I32, name="word_table", align_bytes=64)
         nc.sync.dma_start(word_table[:], x_words[0].rearrange("p c r -> p (c r)").bitcast(I32))
-        w2_first = load_weight(w2, PAIRS[0], "w2_then_gate")
 
-        x_planes = keep.tile([P, 2 * S], U8, name="x_planes", align_bytes=64)
-        nc.vector.memset(x_planes[:].bitcast(I32), 0)
+        heads_plane = keep.tile([P, S], U8, name="heads_plane", align_bytes=64)
+        own_plane = keep.tile([P, S], U8, name="own_plane", align_bytes=64)
+        nc.vector.memset(heads_plane[:].bitcast(I32), 0)
+        nc.vector.memset(own_plane[:].bitcast(I32), 0)
         warm = keep.tile([P, 8], F32, name="warm")
         nc.vector.memset(warm[:], 0.0)
         warm_out = keep.tile([P, 8], F32, name="warm_out")
         nc.scalar.activation(warm_out[:], warm[:], SIGMOID)
 
-        picked_bytes = keep.tile([P, 2 * S], U8, name="picked_bytes", align_bytes=64)
-        nc.vector.tensor_copy(picked_bytes[:, 0:S], byte_table[:].indirect(offs_sb[:]))
-        nc.vector.tensor_copy(picked_bytes[:, S : 2 * S], byte_table[:].indirect(own_sb[:]))
-        for q in range(P // QUAD):
-            nc.sync.dma_start(
-                x_planes[QUAD * q : QUAD * q + 4, :].bitcast(I32),
-                picked_bytes[QUAD * q : QUAD * (q + 1) : BLOCK_P, :].bitcast(I32),
-            )
-        w2_second = load_weight(w2, PAIRS[1], "bytes_then_w2")
+        byte_copy = keep.tile([P, T], U8, name="byte_copy", align_bytes=64)
+        nc.vector.tensor_copy(byte_copy[:].bitcast(I32), byte_table[:].bitcast(I32))
 
-        def deal(copy, dealt, raw, js, ms, ts=slice(0, PACK)):
-            copy(
-                dealt[:, ts, ms, js].rearrange("p t m j -> p m j t"),
-                raw[:].rearrange("p j (m t) -> p m j t", t=PACK)[:, ms, :, ts],
-            )
+        def pick_bytes(table, offsets, plane, name):
+            picked = keep.tile([P, S], U8, name=name, align_bytes=64)
+            nc.vector.tensor_copy(picked[:], table[:].indirect(offsets[:]))
+            for q in range(P // QUAD):
+                nc.sync.dma_start(
+                    plane[QUAD * q : QUAD * q + 4, :].bitcast(I32),
+                    picked[QUAD * q : QUAD * (q + 1) : BLOCK_P, :].bitcast(I32),
+                )
 
-        def quantise(name, dealt, groups):
+        pick_bytes(byte_table, offs_sb, heads_plane, "heads_bytes")
+        w2_first = load_weight(w2, LEFT, "w2_left", 4096)
+        w2_second = load_weight(w2, RIGHT, "w2_right", 0)
+        pick_bytes(byte_copy, own_sb, own_plane, "own_bytes")
+
+        def quantise(name, pieces, groups):
+            dealt = keep.tile([P, PACK, P, PACK], BF16, name=f"{name}_dealt", align_bytes=64)
+            for raw, ms, shares in pieces:
+                for copy, ts in shares:
+                    copy(
+                        dealt[:, ts, ms, :].rearrange("p t m j -> p m j t"),
+                        raw[:].rearrange("p j (m t) -> p m j t", t=PACK)[:, :, :, ts],
+                    )
             codes = keep.tile([P, PACK, P], U32, name=f"{name}_codes", align_bytes=64)
             scales = keep.tile([P, PACK, P], U8, name=f"{name}_scales", align_bytes=64)
             for ts in groups:
@@ -87,75 +98,84 @@ def tile_picked_phmix_sigmoid_po_kernel(
                 )
             return codes, scales
 
-        def product(bank, codes, scales, first, h, ts):
+        def product(bank, weight, words, plane, h, ts):
+            codes, scales = weight
             acc = psum.tile([P, ts.stop - ts.start, PLACES], F32, name=bank, tag=bank)
-            cols = slice(first + h * PLACES, first + (h + 1) * PLACES)
+            cols = slice(h * PLACES, (h + 1) * PLACES)
             for t in range(ts.start, ts.stop):
                 nc.tensor.matmul_mx(
                     out=acc[:, t - ts.start, :],
                     lhsT=codes[:, t, :].bitcast(FP8X4),
                     lhsT_scale=scales[:, t, :],
-                    rhs=picked_words[:, cols].bitcast(FP8X4),
-                    rhs_scale=x_planes[:, cols],
+                    rhs=words[:, cols].bitcast(FP8X4),
+                    rhs_scale=plane[:, cols],
                     start=True,
                     stop=True,
                 )
             return acc
 
-        w1_dealt = keep.tile([P, PACK, P, PACK], BF16, name="w1_dealt", align_bytes=64)
-        deal(nc.scalar.copy, w1_dealt, w1_raw, slice(0, PACK), slice(VECTOR_M, P))
-        deal(nc.vector.tensor_copy, w1_dealt, w1_raw, slice(0, PACK), slice(0, VECTOR_M))
-        w1_codes, w1_scales = quantise("w1", w1_dealt, PAIRS)
+        shared = ((nc.vector.tensor_copy, PAIRS[0]), (nc.scalar.copy, PAIRS[1]))
+        w1_mx = quantise("w1", [(w1_raw, slice(0, P), shared)], PAIRS)
 
-        picked_words = keep.tile([P, 2 * S], U32, name="picked_words", align_bytes=64)
-        nc.vector.tensor_copy(picked_words[:, 0:S], word_table[:].bitcast(U32).indirect(offs_sb[:]))
-        nc.vector.tensor_copy(picked_words[:, S : 2 * S], word_table[:].bitcast(U32).indirect(own_sb[:]))
-
-        w2_dealt = keep.tile([P, PACK, P, PACK], BF16, name="w2_dealt", align_bytes=64)
-        deal(nc.scalar.copy, w2_dealt, w2_first, PAIRS[0], slice(0, P))
-        for ts in PAIRS:
-            deal(nc.vector.tensor_copy, w2_dealt, w2_second, PAIRS[1], slice(0, P), ts)
-        w2_codes, w2_scales = quantise("w2", w2_dealt, FIRST_UNITS)
-
-        gate = keep.tile([P, 2, PACK, PLACES], F32, name="gate", tag="w2_then_gate", align_bytes=64)
+        heads_words = keep.tile([P, S], U32, name="heads_words", align_bytes=64)
+        own_words = keep.tile([P, S], U32, name="own_words", align_bytes=64)
         for h in range(2):
-            for ts in PAIRS:
-                acc = product(f"bank_y_{h}_{ts.start}", w1_codes, w1_scales, 0, h, ts)
-                nc.scalar.activation(gate[:, h, ts, :], acc[:], SIGMOID)
+            nc.vector.tensor_copy(
+                heads_words[:, h * PLACES : (h + 1) * PLACES],
+                word_table[:].bitcast(U32).indirect(offs_sb[:, h * PLACES // 16 : (h + 1) * PLACES // 16]),
+            )
+        nc.vector.tensor_copy(own_words[:], word_table[:].bitcast(U32).indirect(own_sb[:]))
 
+        w2_mx = quantise(
+            "w2",
+            [(w2_first, LEFT, [(nc.scalar.copy, slice(0, PACK))]), (w2_second, RIGHT, [(nc.vector.tensor_copy, ts) for ts in PAIRS])],
+            (slice(0, 1), slice(1, 2), PAIRS[1]),
+        )
+
+        gate = reuse.tile([P, 2, PACK, PLACES], F32, name="gate", offset=6144, align_bytes=64)
+        results = [keep.tile([P, PACK, PLACES], F32, name=f"result_{h}", align_bytes=64) for h in range(2)]
         out_rows = out_0.rearrange("(p t) c -> p t c", t=PACK)
-        out_words = out_1[0].rearrange("p c r -> p (c r)").bitcast(I32)
-        codes = keep.tile([P, S], I32, name="codes", align_bytes=64)
-        scales = keep.tile([P, S], U8, name="scales", align_bytes=64)
 
-        results = []
-        for h in range(2):
-            result = keep.tile([P, PACK, PLACES], F32, name=f"result_{h}", align_bytes=64)
-            results.append(result)
-            for ts in FIRST_UNITS if h == 0 else PAIRS:
-                bank = "bank_y_0_0" if (h, ts.start) == (1, 2) else f"bank_e_{h}_{ts.start}"
-                acc = product(bank, w2_codes, w2_scales, S, h, ts)
-                nc.vector.tensor_tensor(result[:, ts, :], acc[:], gate[:, h, ts, :], MULT)
-                nc.sync.dma_start(out_rows[:, ts, h * PLACES : (h + 1) * PLACES], result[:, ts, :])
+        def heads(bank, h, ts):
+            acc = product(bank, w1_mx, heads_words, heads_plane, h, ts)
+            nc.scalar.activation(gate[:, h, ts, :], acc[:], SIGMOID)
 
-        def interleave(copy, rounded, result, c0, c1):
+        def gated(bank, h, ts):
+            acc = product(bank, w2_mx, own_words, own_plane, h, ts)
+            nc.vector.tensor_tensor(results[h][:, ts, :], acc[:], gate[:, h, ts, :], MULT)
+            nc.sync.dma_start(out_rows[:, ts, h * PLACES : (h + 1) * PLACES], results[h][:, ts, :])
+
+        heads("bank_0", 0, PAIRS[0])
+        heads("bank_1", 0, PAIRS[1])
+        heads("bank_2", 1, PAIRS[0])
+        heads("bank_3", 1, PAIRS[1])
+        gated("bank_4", 0, slice(0, 1))
+        gated("bank_5", 0, slice(1, 2))
+        gated("bank_6", 0, PAIRS[1])
+        gated("bank_4", 1, PAIRS[0])
+        gated("bank_5", 1, PAIRS[1])
+
+        rounded = keep.tile([P, S, PACK], BF16, name="rounded", align_bytes=64)
+
+        def interleave(copy, h, c0, c1):
             copy(
-                rounded[:, c0:c1, :].rearrange("p (c i) t -> p c t i", i=4),
-                result[:, :, c0:c1].rearrange("p t (c i) -> p c t i", i=4),
+                rounded[:, h * PLACES + c0 : h * PLACES + c1, :].rearrange("p (c i) t -> p c t i", i=4),
+                results[h][:, :, c0:c1].rearrange("p t (c i) -> p c t i", i=4),
             )
 
+        interleave(nc.scalar.copy, 0, 0, PLACES)
+        interleave(nc.scalar.copy, 1, 0, SCALAR_PLACES)
+        interleave(nc.vector.tensor_copy, 1, SCALAR_PLACES, PLACES)
+
+        out_words = out_1[0].rearrange("p c r -> p (c r)").bitcast(I32)
+        codes = reuse.tile([P, S], I32, name="codes", offset=12288, align_bytes=64)
+        scales = keep.tile([P, S], U8, name="scales", align_bytes=64)
         for h in range(2):
-            rounded = keep.tile([P, PLACES, PACK], BF16, name=f"rounded_{h}", align_bytes=64)
-            if h == 0:
-                interleave(nc.scalar.copy, rounded, results[h], 0, PLACES)
-            else:
-                interleave(nc.scalar.copy, rounded, results[h], 0, 96)
-                interleave(nc.vector.tensor_copy, rounded, results[h], 96, PLACES)
             cols = slice(h * PLACES, (h + 1) * PLACES)
             nc.vector.quantize_mx(
                 out=codes[:, cols].bitcast(FP8X4),
                 scales=scales[:, cols],
-                in_=rounded[:].rearrange("p c t -> p (c t)"),
+                in_=rounded[:, cols, :].rearrange("p c t -> p (c t)"),
             )
             nc.sync.dma_start(out_words[:, cols], codes[:, cols])
         for q in range(P // QUAD):

@@ -20,9 +20,10 @@ PACK = 4
 QUAD = 32
 BLOCK_P = 8
 PAIRS = (slice(0, 2), slice(2, 4))
-LEFT, RIGHT = slice(0, P // 2), slice(P // 2, P)
-PLACES = S // 2
-SCALAR_PLACES = 80
+SLOTS = slice(0, PACK)
+HALVES = (slice(0, P // 2), slice(P // 2, P))
+PLACES = 128
+UNITS = S // PLACES
 
 
 def tile_picked_phmix_sigmoid_po_kernel(
@@ -37,12 +38,11 @@ def tile_picked_phmix_sigmoid_po_kernel(
 
         offs_sb = lists.tile([P, S // 16], U16, name="offs_sb")
         own_sb = lists.tile([P, S // 16], U16, name="own_sb")
-        nc.sync.dma_start(offs_sb[:], offs)
-        nc.sync.dma_start(own_sb[:], own)
-
-        byte_table = reuse.tile([P, T], U8, name="byte_table", offset=3072, align_bytes=64)
+        byte_table = reuse.tile([P, T], U8, name="byte_table", offset=4096, align_bytes=64)
         scale_rows = x_scales[0].bitcast(I32).unsqueeze(1).to_broadcast([P // BLOCK_P, BLOCK_P, T // 4])
         nc.sync.dma_start(byte_table[:].bitcast(I32), scale_rows)
+        nc.sync.dma_start(offs_sb[:], offs)
+        nc.sync.dma_start(own_sb[:], own)
 
         def load_weight(w, ms, name, offset):
             raw = reuse.tile([P, PACK, PACK * (ms.stop - ms.start)], F32, name=name, offset=offset, align_bytes=64)
@@ -50,58 +50,69 @@ def tile_picked_phmix_sigmoid_po_kernel(
             nc.sync.dma_start(raw[:], rows[:, :, PACK * ms.start : PACK * ms.stop])
             return raw
 
-        w1_raw = load_weight(w1, slice(0, P), "w1_raw", 16384)
         word_table = keep.tile([P, T], I32, name="word_table", align_bytes=64)
         nc.sync.dma_start(word_table[:], x_words[0].rearrange("p c r -> p (c r)").bitcast(I32))
+        w1_raw = [load_weight(w1, ms, f"w1_raw_{i}", 10240 + 4096 * i) for i, ms in enumerate(HALVES)]
 
-        heads_plane = keep.tile([P, S], U8, name="heads_plane", align_bytes=64)
-        own_plane = keep.tile([P, S], U8, name="own_plane", align_bytes=64)
-        nc.vector.memset(heads_plane[:].bitcast(I32), 0)
-        nc.vector.memset(own_plane[:].bitcast(I32), 0)
+        planes = keep.tile([P, 2 * S], U8, name="planes", align_bytes=64)
+        nc.vector.memset(planes[:].bitcast(I32), 0)
+        heads_plane, own_plane = planes[:, 0:S], planes[:, S : 2 * S]
         warm = keep.tile([P, 8], F32, name="warm")
         nc.vector.memset(warm[:], 0.0)
         warm_out = keep.tile([P, 8], F32, name="warm_out")
         nc.scalar.activation(warm_out[:], warm[:], SIGMOID)
 
-        byte_copy = keep.tile([P, T], U8, name="byte_copy", align_bytes=64)
-        nc.vector.tensor_copy(byte_copy[:].bitcast(I32), byte_table[:].bitcast(I32))
+        picked = keep.tile([P, 2 * S], U8, name="picked", align_bytes=64)
+        nc.vector.tensor_copy(picked[:, 0:S], byte_table[:].indirect(offs_sb[:]))
+        nc.vector.tensor_copy(picked[:, S : 2 * S], byte_table[:].indirect(own_sb[:]))
+        for q in range(P // QUAD):
+            nc.sync.dma_start(
+                planes[QUAD * q : QUAD * q + 4, :].bitcast(I32),
+                picked[QUAD * q : QUAD * (q + 1) : BLOCK_P, :].bitcast(I32),
+            )
+        w2_raw = [load_weight(w2, ms, f"w2_raw_{i}", 5120 - 4096 * i) for i, ms in enumerate(HALVES)]
 
-        def pick_bytes(table, offsets, plane, name):
-            picked = keep.tile([P, S], U8, name=name, align_bytes=64)
-            nc.vector.tensor_copy(picked[:], table[:].indirect(offsets[:]))
-            for q in range(P // QUAD):
-                nc.sync.dma_start(
-                    plane[QUAD * q : QUAD * q + 4, :].bitcast(I32),
-                    picked[QUAD * q : QUAD * (q + 1) : BLOCK_P, :].bitcast(I32),
-                )
+        heads_words = keep.tile([P, S], U32, name="heads_words", align_bytes=64)
+        own_words = keep.tile([P, S], U32, name="own_words", align_bytes=64)
+        nc.vector.tensor_copy(heads_words[:], word_table[:].bitcast(U32).indirect(offs_sb[:]))
+        nc.vector.tensor_copy(own_words[:], word_table[:].bitcast(U32).indirect(own_sb[:]))
 
-        pick_bytes(byte_table, offs_sb, heads_plane, "heads_bytes")
-        w2_first = load_weight(w2, LEFT, "w2_left", 4096)
-        w2_second = load_weight(w2, RIGHT, "w2_right", 0)
-        pick_bytes(byte_copy, own_sb, own_plane, "own_bytes")
+        def deal(copy, dealt, raw, ts):
+            copy(
+                dealt.rearrange("p t m j -> p m j t"),
+                raw[:].rearrange("p j (m t) -> p m j t", t=PACK)[:, :, :, ts],
+            )
 
-        def quantise(name, pieces, groups):
-            dealt = keep.tile([P, PACK, P, PACK], BF16, name=f"{name}_dealt", align_bytes=64)
-            for raw, ms, shares in pieces:
-                for copy, ts in shares:
-                    copy(
-                        dealt[:, ts, ms, :].rearrange("p t m j -> p m j t"),
-                        raw[:].rearrange("p j (m t) -> p m j t", t=PACK)[:, :, :, ts],
-                    )
-            codes = keep.tile([P, PACK, P], U32, name=f"{name}_codes", align_bytes=64)
-            scales = keep.tile([P, PACK, P], U8, name=f"{name}_scales", align_bytes=64)
-            for ts in groups:
-                nc.vector.quantize_mx(
-                    out=codes[:, ts, :].rearrange("p t m -> p (t m)").bitcast(FP8X4),
-                    scales=scales[:, ts, :].rearrange("p t m -> p (t m)"),
-                    in_=dealt[:, ts, :, :].rearrange("p t m j -> p (t m j)"),
-                )
-            return codes, scales
+        def quantise(codes, scales, dealt):
+            nc.vector.quantize_mx(out=codes.bitcast(FP8X4), scales=scales, in_=dealt)
 
-        def product(bank, weight, words, plane, h, ts):
-            codes, scales = weight
+        w1_codes = keep.tile([P, PACK, P], U32, name="w1_codes", align_bytes=64)
+        w1_scales = keep.tile([P, PACK, P], U8, name="w1_scales", align_bytes=64)
+        w2_codes = keep.tile([P, PACK, P], U32, name="w2_codes", align_bytes=64)
+        w2_scales = keep.tile([P, PACK, P], U8, name="w2_scales", align_bytes=64)
+
+        w1_dealt = [keep.tile([P, 2, P, PACK], BF16, name=f"w1_dealt_{i}", align_bytes=64) for i in range(2)]
+        for i, ts in enumerate(PAIRS):
+            deal(nc.scalar.copy, w1_dealt[i][:, :, HALVES[0], :], w1_raw[0], ts)
+        deal(nc.vector.tensor_copy, w1_dealt[0][:, :, HALVES[1], :], w1_raw[1], PAIRS[0])
+        deal(nc.scalar.copy, w1_dealt[1][:, :, HALVES[1], :], w1_raw[1], PAIRS[1])
+        for i, ts in enumerate(PAIRS):
+            quantise(
+                w1_codes[:, ts, :].rearrange("p t m -> p (t m)"),
+                w1_scales[:, ts, :].rearrange("p t m -> p (t m)"),
+                w1_dealt[i][:].rearrange("p t m j -> p (t m j)"),
+            )
+
+        for half, ms in enumerate(HALVES):
+            dealt = [keep.tile([P, 2, P // 2, PACK], BF16, name=f"w2_dealt_{half}_{i}", align_bytes=64) for i in range(2)]
+            deal(nc.vector.tensor_copy, dealt[0][:], w2_raw[half], PAIRS[0])
+            deal(nc.scalar.copy, dealt[1][:], w2_raw[half], PAIRS[1])
+            for t in range(PACK):
+                quantise(w2_codes[:, t, ms], w2_scales[:, t, ms], dealt[t // 2][:, t % 2, :, :].rearrange("p m j -> p (m j)"))
+
+        def product(bank, codes, scales, words, plane, c, ts):
             acc = psum.tile([P, ts.stop - ts.start, PLACES], F32, name=bank, tag=bank)
-            cols = slice(h * PLACES, (h + 1) * PLACES)
+            cols = slice(c * PLACES, (c + 1) * PLACES)
             for t in range(ts.start, ts.stop):
                 nc.tensor.matmul_mx(
                     out=acc[:, t - ts.start, :],
@@ -114,69 +125,49 @@ def tile_picked_phmix_sigmoid_po_kernel(
                 )
             return acc
 
-        shared = ((nc.vector.tensor_copy, PAIRS[0]), (nc.scalar.copy, PAIRS[1]))
-        w1_mx = quantise("w1", [(w1_raw, slice(0, P), shared)], PAIRS)
-
-        heads_words = keep.tile([P, S], U32, name="heads_words", align_bytes=64)
-        own_words = keep.tile([P, S], U32, name="own_words", align_bytes=64)
-        for h in range(2):
-            nc.vector.tensor_copy(
-                heads_words[:, h * PLACES : (h + 1) * PLACES],
-                word_table[:].bitcast(U32).indirect(offs_sb[:, h * PLACES // 16 : (h + 1) * PLACES // 16]),
-            )
-        nc.vector.tensor_copy(own_words[:], word_table[:].bitcast(U32).indirect(own_sb[:]))
-
-        w2_mx = quantise(
-            "w2",
-            [(w2_first, LEFT, [(nc.scalar.copy, slice(0, PACK))]), (w2_second, RIGHT, [(nc.vector.tensor_copy, ts) for ts in PAIRS])],
-            (slice(0, 1), slice(1, 2), PAIRS[1]),
-        )
-
-        gate = reuse.tile([P, 2, PACK, PLACES], F32, name="gate", offset=6144, align_bytes=64)
-        results = [keep.tile([P, PACK, PLACES], F32, name=f"result_{h}", align_bytes=64) for h in range(2)]
+        gates = [reuse.tile([P, PACK, PLACES], F32, name=f"gate_{c}", offset=2048 * ((c - 1) % UNITS), align_bytes=64) for c in range(UNITS)]
+        results = [keep.tile([P, PACK, PLACES], F32, name=f"result_{c}", align_bytes=64) for c in range(UNITS)]
         out_rows = out_0.rearrange("(p t) c -> p t c", t=PACK)
 
-        def heads(bank, h, ts):
-            acc = product(bank, w1_mx, heads_words, heads_plane, h, ts)
-            nc.scalar.activation(gate[:, h, ts, :], acc[:], SIGMOID)
+        def heads(bank, c):
+            acc = product(bank, w1_codes, w1_scales, heads_words, heads_plane, c, SLOTS)
+            nc.scalar.activation(gates[c][:], acc[:], SIGMOID)
 
-        def gated(bank, h, ts):
-            acc = product(bank, w2_mx, own_words, own_plane, h, ts)
-            nc.vector.tensor_tensor(results[h][:, ts, :], acc[:], gate[:, h, ts, :], MULT)
-            nc.sync.dma_start(out_rows[:, ts, h * PLACES : (h + 1) * PLACES], results[h][:, ts, :])
+        def gated(bank, c, ts):
+            acc = product(bank, w2_codes, w2_scales, own_words, own_plane, c, ts)
+            nc.vector.tensor_tensor(results[c][:, ts, :], acc[:], gates[c][:, ts, :], MULT)
 
-        heads("bank_0", 0, PAIRS[0])
-        heads("bank_1", 0, PAIRS[1])
-        heads("bank_2", 1, PAIRS[0])
-        heads("bank_3", 1, PAIRS[1])
-        gated("bank_4", 0, slice(0, 1))
-        gated("bank_5", 0, slice(1, 2))
-        gated("bank_6", 0, PAIRS[1])
-        gated("bank_4", 1, PAIRS[0])
-        gated("bank_5", 1, PAIRS[1])
+        def store(c):
+            nc.sync.dma_start(out_rows[:, :, c * PLACES : (c + 1) * PLACES], results[c][:])
 
-        rounded = keep.tile([P, S, PACK], BF16, name="rounded", align_bytes=64)
+        for c in range(UNITS):
+            heads(f"bank_{c}", c)
+        gated("bank_4", 0, PAIRS[0])
+        gated("bank_0", 0, PAIRS[1])
+        store(0)
+        for c in range(1, UNITS):
+            gated(f"bank_{4 + c}", c, SLOTS)
+            store(c)
 
-        def interleave(copy, h, c0, c1):
+        rounded = [keep.tile([P, 2 * PLACES, PACK], BF16, name=f"rounded_{h}", align_bytes=64) for h in range(2)]
+
+        def interleave(copy, c, c0, c1):
+            first = c % 2 * PLACES
             copy(
-                rounded[:, h * PLACES + c0 : h * PLACES + c1, :].rearrange("p (c i) t -> p c t i", i=4),
-                results[h][:, :, c0:c1].rearrange("p t (c i) -> p c t i", i=4),
+                rounded[c // 2][:, first + c0 : first + c1, :].rearrange("p (c i) t -> p c t i", i=4),
+                results[c][:, :, c0:c1].rearrange("p t (c i) -> p c t i", i=4),
             )
 
-        interleave(nc.scalar.copy, 0, 0, PLACES)
-        interleave(nc.scalar.copy, 1, 0, SCALAR_PLACES)
-        interleave(nc.vector.tensor_copy, 1, SCALAR_PLACES, PLACES)
+        for c in range(UNITS - 1):
+            interleave(nc.scalar.copy, c, 0, PLACES)
+        interleave(nc.vector.tensor_copy, UNITS - 1, 0, PLACES)
 
         out_words = out_1[0].rearrange("p c r -> p (c r)").bitcast(I32)
-        codes = reuse.tile([P, S], I32, name="codes", offset=12288, align_bytes=64)
+        codes = reuse.tile([P, S], I32, name="codes", offset=4096, align_bytes=64)
         scales = keep.tile([P, S], U8, name="scales", align_bytes=64)
         for h in range(2):
-            cols = slice(h * PLACES, (h + 1) * PLACES)
-            nc.vector.quantize_mx(
-                out=codes[:, cols].bitcast(FP8X4),
-                scales=scales[:, cols],
-                in_=rounded[:, cols, :].rearrange("p c t -> p (c t)"),
-            )
+            cols = slice(2 * h * PLACES, 2 * (h + 1) * PLACES)
+            quantise(codes[:, cols], scales[:, cols], rounded[h][:].rearrange("p c t -> p (c t)"))
             nc.sync.dma_start(out_words[:, cols], codes[:, cols])
         for q in range(P // QUAD):
             queue = nc.scalar if q % 2 else nc.sync

@@ -24,6 +24,7 @@ SLOTS = slice(0, PACK)
 HALVES = (slice(0, P // 2), slice(P // 2, P))
 PLACES = 128
 UNITS = S // PLACES
+FIRST = 512
 
 
 def tile_picked_phmix_sigmoid_po_kernel(
@@ -38,11 +39,15 @@ def tile_picked_phmix_sigmoid_po_kernel(
 
         offs_sb = lists.tile([P, S // 16], U16, name="offs_sb")
         own_sb = lists.tile([P, S // 16], U16, name="own_sb")
-        byte_table = reuse.tile([P, T], U8, name="byte_table", offset=4096, align_bytes=64)
-        scale_rows = x_scales[0].bitcast(I32).unsqueeze(1).to_broadcast([P // BLOCK_P, BLOCK_P, T // 4])
-        nc.sync.dma_start(byte_table[:].bitcast(I32), scale_rows)
+        byte_table = reuse.tile([P, T], U8, name="byte_table", offset=18432, align_bytes=64)
+        nc.vector.memset(byte_table[:].bitcast(I32), 0)
+        word_table = keep.tile([P, T], I32, name="word_table", align_bytes=64)
+        word_rows = x_words[0].rearrange("p c r -> p (c r)").bitcast(I32)
+        nc.sync.dma_start(word_table[:, 0:FIRST], word_rows[:, 0:FIRST])
         nc.sync.dma_start(offs_sb[:], offs)
         nc.sync.dma_start(own_sb[:], own)
+        nc.sync.dma_start(byte_table[0:P:BLOCK_P, :].bitcast(I32), x_scales[0].bitcast(I32))
+        nc.sync.dma_start(word_table[:, FIRST:T], word_rows[:, FIRST:T])
 
         def load_weight(w, ms, name, offset):
             raw = reuse.tile([P, PACK, PACK * (ms.stop - ms.start)], F32, name=name, offset=offset, align_bytes=64)
@@ -50,27 +55,30 @@ def tile_picked_phmix_sigmoid_po_kernel(
             nc.sync.dma_start(raw[:], rows[:, :, PACK * ms.start : PACK * ms.stop])
             return raw
 
-        word_table = keep.tile([P, T], I32, name="word_table", align_bytes=64)
-        nc.sync.dma_start(word_table[:], x_words[0].rearrange("p c r -> p (c r)").bitcast(I32))
         w1_raw = [load_weight(w1, ms, f"w1_raw_{i}", 10240 + 4096 * i) for i, ms in enumerate(HALVES)]
 
-        planes = keep.tile([P, 2 * S], U8, name="planes", align_bytes=64)
-        nc.vector.memset(planes[:].bitcast(I32), 0)
-        heads_plane, own_plane = planes[:, 0:S], planes[:, S : 2 * S]
+        heads_plane = keep.tile([P, S], U8, name="heads_plane", align_bytes=64)
+        own_plane = keep.tile([P, S], U8, name="own_plane", align_bytes=64)
+        nc.vector.memset(heads_plane[:].bitcast(I32), 0)
+        nc.vector.memset(own_plane[:].bitcast(I32), 0)
         warm = keep.tile([P, 8], F32, name="warm")
         nc.vector.memset(warm[:], 0.0)
         warm_out = keep.tile([P, 8], F32, name="warm_out")
         nc.scalar.activation(warm_out[:], warm[:], SIGMOID)
 
-        picked = keep.tile([P, 2 * S], U8, name="picked", align_bytes=64)
-        nc.vector.tensor_copy(picked[:, 0:S], byte_table[:].indirect(offs_sb[:]))
-        nc.vector.tensor_copy(picked[:, S : 2 * S], byte_table[:].indirect(own_sb[:]))
-        for q in range(P // QUAD):
-            nc.sync.dma_start(
-                planes[QUAD * q : QUAD * q + 4, :].bitcast(I32),
-                picked[QUAD * q : QUAD * (q + 1) : BLOCK_P, :].bitcast(I32),
-            )
-        w2_raw = [load_weight(w2, ms, f"w2_raw_{i}", 5120 - 4096 * i) for i, ms in enumerate(HALVES)]
+        def pick_bytes(offsets, plane, name):
+            picked = keep.tile([P, S], U8, name=name, align_bytes=64)
+            nc.vector.tensor_copy(picked[:], byte_table[:].indirect(offsets[:]))
+            for q in range(P // QUAD):
+                nc.sync.dma_start(
+                    plane[QUAD * q : QUAD * q + 4, :].bitcast(I32),
+                    picked[QUAD * q : QUAD * (q + 1) : BLOCK_P, :].bitcast(I32),
+                )
+
+        w2_raw = [load_weight(w2, HALVES[0], "w2_raw_0", 5120)]
+        pick_bytes(offs_sb, heads_plane, "heads_bytes")
+        w2_raw.append(load_weight(w2, HALVES[1], "w2_raw_1", 1024))
+        pick_bytes(own_sb, own_plane, "own_bytes")
 
         heads_words = keep.tile([P, S], U32, name="heads_words", align_bytes=64)
         own_words = keep.tile([P, S], U32, name="own_words", align_bytes=64)
@@ -91,24 +99,25 @@ def tile_picked_phmix_sigmoid_po_kernel(
         w2_codes = keep.tile([P, PACK, P], U32, name="w2_codes", align_bytes=64)
         w2_scales = keep.tile([P, PACK, P], U8, name="w2_scales", align_bytes=64)
 
-        w1_dealt = [keep.tile([P, 2, P, PACK], BF16, name=f"w1_dealt_{i}", align_bytes=64) for i in range(2)]
-        for i, ts in enumerate(PAIRS):
-            deal(nc.scalar.copy, w1_dealt[i][:, :, HALVES[0], :], w1_raw[0], ts)
-        deal(nc.vector.tensor_copy, w1_dealt[0][:, :, HALVES[1], :], w1_raw[1], PAIRS[0])
-        deal(nc.scalar.copy, w1_dealt[1][:, :, HALVES[1], :], w1_raw[1], PAIRS[1])
-        for i, ts in enumerate(PAIRS):
-            quantise(
-                w1_codes[:, ts, :].rearrange("p t m -> p (t m)"),
-                w1_scales[:, ts, :].rearrange("p t m -> p (t m)"),
-                w1_dealt[i][:].rearrange("p t m j -> p (t m j)"),
-            )
+        def quantise_weight(codes, scales, dealt):
+            for i, ts in enumerate(PAIRS):
+                quantise(
+                    codes[:, ts, :].rearrange("p t m -> p (t m)"),
+                    scales[:, ts, :].rearrange("p t m -> p (t m)"),
+                    dealt[i][:].rearrange("p t m j -> p (t m j)"),
+                )
 
+        w1_dealt = [keep.tile([P, 2, P, PACK], BF16, name=f"w1_dealt_{i}", align_bytes=64) for i in range(2)]
         for half, ms in enumerate(HALVES):
-            dealt = [keep.tile([P, 2, P // 2, PACK], BF16, name=f"w2_dealt_{half}_{i}", align_bytes=64) for i in range(2)]
-            deal(nc.vector.tensor_copy, dealt[0][:], w2_raw[half], PAIRS[0])
-            deal(nc.scalar.copy, dealt[1][:], w2_raw[half], PAIRS[1])
-            for t in range(PACK):
-                quantise(w2_codes[:, t, ms], w2_scales[:, t, ms], dealt[t // 2][:, t % 2, :, :].rearrange("p m j -> p (m j)"))
+            for i, ts in enumerate(PAIRS):
+                deal(nc.scalar.copy, w1_dealt[i][:, :, ms, :], w1_raw[half], ts)
+        quantise_weight(w1_codes, w1_scales, w1_dealt)
+
+        w2_dealt = [keep.tile([P, 2, P, PACK], BF16, name=f"w2_dealt_{i}", align_bytes=64) for i in range(2)]
+        for half, copy in enumerate((nc.scalar.copy, nc.vector.tensor_copy)):
+            for i, ts in enumerate(PAIRS):
+                deal(copy, w2_dealt[i][:, :, HALVES[half], :], w2_raw[half], ts)
+        quantise_weight(w2_codes, w2_scales, w2_dealt)
 
         def product(bank, codes, scales, words, plane, c, ts):
             acc = psum.tile([P, ts.stop - ts.start, PLACES], F32, name=bank, tag=bank)

@@ -14,16 +14,18 @@ U8 = mybir.dt.uint8
 FP8X4 = mybir.dt.float8_e4m3fn_x4
 SIGMOID = mybir.ActivationFunctionType.Sigmoid
 MULT = mybir.AluOpType.mult
+ADD = mybir.AluOpType.add
 
 P = 128
 PACK = 4
 QUAD = 32
 BLOCK_P = 8
 PAIRS = (slice(0, 2), slice(2, 4))
-SLOTS = slice(0, PACK)
 HALVES = (slice(0, P // 2), slice(P // 2, P))
-PLACES = 128
-UNITS = S // PLACES
+SLOTS = slice(0, PACK)
+PLACES = S // 2
+SCALAR_PLACES = 96
+POOL_PLACES = 112
 FIRST = 512
 
 
@@ -39,7 +41,7 @@ def tile_picked_phmix_sigmoid_po_kernel(
 
         offs_sb = lists.tile([P, S // 16], U16, name="offs_sb")
         own_sb = lists.tile([P, S // 16], U16, name="own_sb")
-        byte_table = reuse.tile([P, T], U8, name="byte_table", offset=18432, align_bytes=64)
+        byte_table = reuse.tile([P, T], U8, name="byte_table", offset=24576, align_bytes=64)
         nc.vector.memset(byte_table[:].bitcast(I32), 0)
         word_table = keep.tile([P, T], I32, name="word_table", align_bytes=64)
         word_rows = x_words[0].rearrange("p c r -> p (c r)").bitcast(I32)
@@ -47,7 +49,8 @@ def tile_picked_phmix_sigmoid_po_kernel(
         nc.sync.dma_start(offs_sb[:], offs)
         nc.sync.dma_start(own_sb[:], own)
         nc.sync.dma_start(byte_table[0:P:BLOCK_P, :].bitcast(I32), x_scales[0].bitcast(I32))
-        nc.sync.dma_start(word_table[:, FIRST:T], word_rows[:, FIRST:T])
+        for cols in (slice(FIRST, (FIRST + T) // 2), slice((FIRST + T) // 2, T)):
+            nc.sync.dma_start(word_table[:, cols], word_rows[:, cols])
 
         def load_weight(w, ms, name, offset):
             raw = reuse.tile([P, PACK, PACK * (ms.stop - ms.start)], F32, name=name, offset=offset, align_bytes=64)
@@ -55,7 +58,7 @@ def tile_picked_phmix_sigmoid_po_kernel(
             nc.sync.dma_start(raw[:], rows[:, :, PACK * ms.start : PACK * ms.stop])
             return raw
 
-        w1_raw = [load_weight(w1, ms, f"w1_raw_{i}", 10240 + 4096 * i) for i, ms in enumerate(HALVES)]
+        w1_raw = [load_weight(w1, ms, f"w1_raw_{i}", 16384 + 4096 * i) for i, ms in enumerate(HALVES)]
 
         heads_plane = keep.tile([P, S], U8, name="heads_plane", align_bytes=64)
         own_plane = keep.tile([P, S], U8, name="own_plane", align_bytes=64)
@@ -75,9 +78,8 @@ def tile_picked_phmix_sigmoid_po_kernel(
                     picked[QUAD * q : QUAD * (q + 1) : BLOCK_P, :].bitcast(I32),
                 )
 
-        w2_raw = [load_weight(w2, HALVES[0], "w2_raw_0", 5120)]
         pick_bytes(offs_sb, heads_plane, "heads_bytes")
-        w2_raw.append(load_weight(w2, HALVES[1], "w2_raw_1", 1024))
+        w2_raw = [load_weight(w2, ms, f"w2_raw_{i}", 5120 - 4096 * i) for i, ms in enumerate(HALVES)]
         pick_bytes(own_sb, own_plane, "own_bytes")
 
         heads_words = keep.tile([P, S], U32, name="heads_words", align_bytes=64)
@@ -100,28 +102,31 @@ def tile_picked_phmix_sigmoid_po_kernel(
         w2_scales = keep.tile([P, PACK, P], U8, name="w2_scales", align_bytes=64)
 
         def quantise_weight(codes, scales, dealt):
-            for i, ts in enumerate(PAIRS):
+            for ts in PAIRS:
                 quantise(
                     codes[:, ts, :].rearrange("p t m -> p (t m)"),
                     scales[:, ts, :].rearrange("p t m -> p (t m)"),
-                    dealt[i][:].rearrange("p t m j -> p (t m j)"),
+                    dealt[:, ts, :, :].rearrange("p t m j -> p (t m j)"),
                 )
 
-        w1_dealt = [keep.tile([P, 2, P, PACK], BF16, name=f"w1_dealt_{i}", align_bytes=64) for i in range(2)]
-        for half, ms in enumerate(HALVES):
-            for i, ts in enumerate(PAIRS):
-                deal(nc.scalar.copy, w1_dealt[i][:, :, ms, :], w1_raw[half], ts)
+        w1_dealt = keep.tile([P, PACK, P, PACK], BF16, name="w1_dealt", align_bytes=64)
+        deal(nc.scalar.copy, w1_dealt[:, :, HALVES[0], :], w1_raw[0], SLOTS)
+        for ts in PAIRS:
+            deal(nc.scalar.copy, w1_dealt[:, ts, HALVES[1], :], w1_raw[1], ts)
         quantise_weight(w1_codes, w1_scales, w1_dealt)
 
-        w2_dealt = [keep.tile([P, 2, P, PACK], BF16, name=f"w2_dealt_{i}", align_bytes=64) for i in range(2)]
-        for half, copy in enumerate((nc.scalar.copy, nc.vector.tensor_copy)):
-            for i, ts in enumerate(PAIRS):
-                deal(copy, w2_dealt[i][:, :, HALVES[half], :], w2_raw[half], ts)
+        w2_dealt = keep.tile([P, PACK, P, PACK], BF16, name="w2_dealt", align_bytes=64)
+        for ms, raw in zip(HALVES, w2_raw):
+            for copy, ts in zip((nc.vector.tensor_copy, nc.scalar.copy), PAIRS):
+                deal(copy, w2_dealt[:, ts, ms, :], raw, ts)
         quantise_weight(w2_codes, w2_scales, w2_dealt)
 
-        def product(bank, codes, scales, words, plane, c, ts):
+        w1_mx, w2_mx = (w1_codes, w1_scales), (w2_codes, w2_scales)
+
+        def product(bank, weight, words, plane, h, ts):
+            codes, scales = weight
             acc = psum.tile([P, ts.stop - ts.start, PLACES], F32, name=bank, tag=bank)
-            cols = slice(c * PLACES, (c + 1) * PLACES)
+            cols = slice(h * PLACES, (h + 1) * PLACES)
             for t in range(ts.start, ts.stop):
                 nc.tensor.matmul_mx(
                     out=acc[:, t - ts.start, :],
@@ -134,49 +139,56 @@ def tile_picked_phmix_sigmoid_po_kernel(
                 )
             return acc
 
-        gates = [reuse.tile([P, PACK, PLACES], F32, name=f"gate_{c}", offset=2048 * ((c - 1) % UNITS), align_bytes=64) for c in range(UNITS)]
-        results = [keep.tile([P, PACK, PLACES], F32, name=f"result_{c}", align_bytes=64) for c in range(UNITS)]
+        gate = reuse.tile([P, 2, PACK, PLACES], F32, name="gate", offset=0, align_bytes=64)
+        results = [keep.tile([P, PACK, PLACES], F32, name=f"result_{h}", align_bytes=64) for h in range(2)]
         out_rows = out_0.rearrange("(p t) c -> p t c", t=PACK)
 
-        def heads(bank, c):
-            acc = product(bank, w1_codes, w1_scales, heads_words, heads_plane, c, SLOTS)
-            nc.scalar.activation(gates[c][:], acc[:], SIGMOID)
+        def heads(bank, h, ts):
+            acc = product(bank, w1_mx, heads_words, heads_plane, h, ts)
+            nc.scalar.activation(gate[:, h, ts, :], acc[:], SIGMOID)
 
-        def gated(bank, c, ts):
-            acc = product(bank, w2_codes, w2_scales, own_words, own_plane, c, ts)
-            nc.vector.tensor_tensor(results[c][:, ts, :], acc[:], gates[c][:, ts, :], MULT)
+        def gated(bank, h, ts):
+            acc = product(bank, w2_mx, own_words, own_plane, h, ts)
+            nc.vector.tensor_tensor(results[h][:, ts, :], acc[:], gate[:, h, ts, :], MULT)
+            nc.sync.dma_start(out_rows[:, ts, h * PLACES : (h + 1) * PLACES], results[h][:, ts, :])
 
-        def store(c):
-            nc.sync.dma_start(out_rows[:, :, c * PLACES : (c + 1) * PLACES], results[c][:])
+        heads("bank_0", 0, slice(0, 1))
+        heads("bank_7", 0, slice(1, 2))
+        heads("bank_1", 0, PAIRS[1])
+        heads("bank_2", 1, PAIRS[0])
+        heads("bank_3", 1, PAIRS[1])
+        gated("bank_4", 0, slice(0, 1))
+        gated("bank_5", 0, slice(1, 2))
+        gated("bank_6", 0, PAIRS[1])
+        gated("bank_4", 1, PAIRS[0])
+        gated("bank_5", 1, PAIRS[1])
 
-        for c in range(UNITS):
-            heads(f"bank_{c}", c)
-        gated("bank_4", 0, PAIRS[0])
-        gated("bank_0", 0, PAIRS[1])
-        store(0)
-        for c in range(1, UNITS):
-            gated(f"bank_{4 + c}", c, SLOTS)
-            store(c)
+        rounded = keep.tile([P, S, PACK], BF16, name="rounded", align_bytes=64)
 
-        rounded = [keep.tile([P, 2 * PLACES, PACK], BF16, name=f"rounded_{h}", align_bytes=64) for h in range(2)]
-
-        def interleave(copy, c, c0, c1):
-            first = c % 2 * PLACES
+        def interleave(copy, h, c0, c1):
             copy(
-                rounded[c // 2][:, first + c0 : first + c1, :].rearrange("p (c i) t -> p c t i", i=4),
-                results[c][:, :, c0:c1].rearrange("p t (c i) -> p c t i", i=4),
+                rounded[:, h * PLACES + c0 : h * PLACES + c1, :].rearrange("p (c i) t -> p c t i", i=4),
+                results[h][:, :, c0:c1].rearrange("p t (c i) -> p c t i", i=4),
             )
 
-        for c in range(UNITS - 1):
-            interleave(nc.scalar.copy, c, 0, PLACES)
-        interleave(nc.vector.tensor_copy, UNITS - 1, 0, PLACES)
+        def pool_copy(out, in_):
+            nc.gpsimd.tensor_scalar(out, in_, 1.0, -0.0, MULT, ADD)
+
+        interleave(pool_copy, 0, 0, POOL_PLACES)
+        interleave(nc.scalar.copy, 0, POOL_PLACES, PLACES)
+        interleave(nc.scalar.copy, 1, 0, SCALAR_PLACES)
+        interleave(nc.vector.tensor_copy, 1, SCALAR_PLACES, PLACES)
 
         out_words = out_1[0].rearrange("p c r -> p (c r)").bitcast(I32)
-        codes = reuse.tile([P, S], I32, name="codes", offset=4096, align_bytes=64)
+        codes = reuse.tile([P, S], I32, name="codes", offset=6144, align_bytes=64)
         scales = keep.tile([P, S], U8, name="scales", align_bytes=64)
         for h in range(2):
-            cols = slice(2 * h * PLACES, 2 * (h + 1) * PLACES)
-            quantise(codes[:, cols], scales[:, cols], rounded[h][:].rearrange("p c t -> p (c t)"))
+            cols = slice(h * PLACES, (h + 1) * PLACES)
+            nc.vector.quantize_mx(
+                out=codes[:, cols].bitcast(FP8X4),
+                scales=scales[:, cols],
+                in_=rounded[:, cols, :].rearrange("p c t -> p (c t)"),
+            )
             nc.sync.dma_start(out_words[:, cols], codes[:, cols])
         for q in range(P // QUAD):
             queue = nc.scalar if q % 2 else nc.sync

@@ -24,8 +24,8 @@ PAIRS = (slice(0, 2), slice(2, 4))
 HALVES = (slice(0, P // 2), slice(P // 2, P))
 SLOTS = slice(0, PACK)
 PLACES = S // 2
-SCALAR_PLACES = 96
-POOL_PLACES = 112
+SCALAR_PLACES = 112
+POOL_PLACES = 128
 FIRST = 512
 
 
@@ -49,16 +49,20 @@ def tile_picked_phmix_sigmoid_po_kernel(
         nc.sync.dma_start(offs_sb[:], offs)
         nc.sync.dma_start(own_sb[:], own)
         nc.sync.dma_start(byte_table[0:P:BLOCK_P, :].bitcast(I32), x_scales[0].bitcast(I32))
-        for cols in (slice(FIRST, (FIRST + T) // 2), slice((FIRST + T) // 2, T)):
-            nc.sync.dma_start(word_table[:, cols], word_rows[:, cols])
+        nc.sync.dma_start(word_table[:, FIRST:T], word_rows[:, FIRST:T])
 
-        def load_weight(w, ms, name, offset):
-            raw = reuse.tile([P, PACK, PACK * (ms.stop - ms.start)], F32, name=name, offset=offset, align_bytes=64)
+        def raw_half(name, offset):
+            return reuse.tile([P, PACK, N // 2], F32, name=name, offset=offset, align_bytes=64)
+
+        def load_half(raw, w, half, js):
             rows = w.rearrange("(p j) c -> p j c", j=PACK)
-            nc.sync.dma_start(raw[:], rows[:, :, PACK * ms.start : PACK * ms.stop])
-            return raw
+            nc.sync.dma_start(raw[:, js, :], rows[:, js, half * N // 2 : (half + 1) * N // 2])
 
-        w1_raw = [load_weight(w1, ms, f"w1_raw_{i}", 16384 + 4096 * i) for i, ms in enumerate(HALVES)]
+        w1_raw = [raw_half(f"w1_raw_{i}", 16384 + 4096 * i) for i in range(2)]
+        w2_raw = [raw_half(f"w2_raw_{i}", 5120 - 4096 * i) for i in range(2)]
+        for half in range(2):
+            load_half(w1_raw[half], w1, half, SLOTS)
+        load_half(w2_raw[0], w2, 0, PAIRS[0])
 
         heads_plane = keep.tile([P, S], U8, name="heads_plane", align_bytes=64)
         own_plane = keep.tile([P, S], U8, name="own_plane", align_bytes=64)
@@ -79,7 +83,8 @@ def tile_picked_phmix_sigmoid_po_kernel(
                 )
 
         pick_bytes(offs_sb, heads_plane, "heads_bytes")
-        w2_raw = [load_weight(w2, ms, f"w2_raw_{i}", 5120 - 4096 * i) for i, ms in enumerate(HALVES)]
+        load_half(w2_raw[0], w2, 0, PAIRS[1])
+        load_half(w2_raw[1], w2, 1, SLOTS)
         pick_bytes(own_sb, own_plane, "own_bytes")
 
         heads_words = keep.tile([P, S], U32, name="heads_words", align_bytes=64)
@@ -160,8 +165,8 @@ def tile_picked_phmix_sigmoid_po_kernel(
         gated("bank_4", 0, slice(0, 1))
         gated("bank_5", 0, slice(1, 2))
         gated("bank_6", 0, PAIRS[1])
-        gated("bank_4", 1, PAIRS[0])
-        gated("bank_5", 1, PAIRS[1])
+        gated("bank_0", 1, PAIRS[0])
+        gated("bank_7", 1, PAIRS[1])
 
         rounded = keep.tile([P, S, PACK], BF16, name="rounded", align_bytes=64)
 
@@ -174,7 +179,7 @@ def tile_picked_phmix_sigmoid_po_kernel(
         def pool_copy(out, in_):
             nc.gpsimd.tensor_scalar(out, in_, 1.0, -0.0, MULT, ADD)
 
-        interleave(pool_copy, 0, 0, POOL_PLACES)
+        pool_copy(rounded[:, 0:POOL_PLACES, :], results[0][:, :, 0:POOL_PLACES].rearrange("p t c -> p c t"))
         interleave(nc.scalar.copy, 0, POOL_PLACES, PLACES)
         interleave(nc.scalar.copy, 1, 0, SCALAR_PLACES)
         interleave(nc.vector.tensor_copy, 1, SCALAR_PLACES, PLACES)

@@ -120,11 +120,12 @@ def tile_picked_phmix_sigmoid_po_kernel(
             deal(nc.scalar.copy, w1_dealt[:, ts, HALVES[1], :], w1_raw[1], ts)
         quantise_weight(w1_codes, w1_scales, w1_dealt)
 
-        w2_dealt = keep.tile([P, PACK, P, PACK], BF16, name="w2_dealt", align_bytes=64)
-        for ms, raw in zip(HALVES, w2_raw):
+        for half, (ms, raw) in enumerate(zip(HALVES, w2_raw)):
+            dealt = keep.tile([P, PACK, P // 2, PACK], BF16, name=f"w2_dealt_{half}", align_bytes=64)
             for copy, ts in zip((nc.vector.tensor_copy, nc.scalar.copy), PAIRS):
-                deal(copy, w2_dealt[:, ts, ms, :], raw, ts)
-        quantise_weight(w2_codes, w2_scales, w2_dealt)
+                deal(copy, dealt[:, ts, :, :], raw, ts)
+            for t in range(PACK):
+                quantise(w2_codes[:, t, ms], w2_scales[:, t, ms], dealt[:, t, :, :].rearrange("p m j -> p (m j)"))
 
         w1_mx, w2_mx = (w1_codes, w1_scales), (w2_codes, w2_scales)
 
@@ -148,25 +149,30 @@ def tile_picked_phmix_sigmoid_po_kernel(
         results = [keep.tile([P, PACK, PLACES], F32, name=f"result_{h}", align_bytes=64) for h in range(2)]
         out_rows = out_0.rearrange("(p t) c -> p t c", t=PACK)
 
-        def heads(bank, h, ts):
-            acc = product(bank, w1_mx, heads_words, heads_plane, h, ts)
-            nc.scalar.activation(gate[:, h, ts, :], acc[:], SIGMOID)
+        def steps(ts, step):
+            return [(slice(t, t + step), slice(t - ts.start, t - ts.start + step)) for t in range(ts.start, ts.stop, step)]
 
-        def gated(bank, h, ts):
+        def heads(bank, h, ts, step=2):
+            acc = product(bank, w1_mx, heads_words, heads_plane, h, ts)
+            for slots, rows in steps(ts, min(step, ts.stop - ts.start)):
+                nc.scalar.activation(gate[:, h, slots, :], acc[:, rows, :], SIGMOID)
+
+        def gated(bank, h, ts, step=2):
             acc = product(bank, w2_mx, own_words, own_plane, h, ts)
-            nc.vector.tensor_tensor(results[h][:, ts, :], acc[:], gate[:, h, ts, :], MULT)
+            for slots, rows in steps(ts, min(step, ts.stop - ts.start)):
+                nc.vector.tensor_tensor(results[h][:, slots, :], acc[:, rows, :], gate[:, h, slots, :], MULT)
             nc.sync.dma_start(out_rows[:, ts, h * PLACES : (h + 1) * PLACES], results[h][:, ts, :])
 
         heads("bank_0", 0, slice(0, 1))
         heads("bank_7", 0, slice(1, 2))
-        heads("bank_1", 0, PAIRS[1])
-        heads("bank_2", 1, PAIRS[0])
-        heads("bank_3", 1, PAIRS[1])
+        heads("bank_1", 0, PAIRS[1], 1)
+        heads("bank_2", 1, PAIRS[0], 1)
+        heads("bank_3", 1, PAIRS[1], 1)
         gated("bank_4", 0, slice(0, 1))
         gated("bank_5", 0, slice(1, 2))
-        gated("bank_6", 0, PAIRS[1])
-        gated("bank_0", 1, PAIRS[0])
-        gated("bank_7", 1, PAIRS[1])
+        gated("bank_6", 0, PAIRS[1], 1)
+        gated("bank_0", 1, PAIRS[0], 1)
+        gated("bank_7", 1, PAIRS[1], 1)
 
         rounded = keep.tile([P, S, PACK], BF16, name="rounded", align_bytes=64)
 

@@ -24,8 +24,8 @@ PAIRS = (slice(0, 2), slice(2, 4))
 HALVES = (slice(0, P // 2), slice(P // 2, P))
 SLOTS = slice(0, PACK)
 PLACES = S // 2
-SCALAR_PLACES = 112
-POOL_PLACES = 128
+SCALAR_PLACES = 96
+POOL_PLACES = 176
 FIRST = 512
 
 
@@ -120,9 +120,9 @@ def tile_picked_phmix_sigmoid_po_kernel(
             deal(nc.scalar.copy, w1_dealt[:, ts, HALVES[1], :], w1_raw[1], ts)
         quantise_weight(w1_codes, w1_scales, w1_dealt)
 
-        for half, (ms, raw) in enumerate(zip(HALVES, w2_raw)):
+        for half, (ms, raw, first) in enumerate(zip(HALVES, w2_raw, (nc.scalar.copy, nc.vector.tensor_copy))):
             dealt = keep.tile([P, PACK, P // 2, PACK], BF16, name=f"w2_dealt_{half}", align_bytes=64)
-            for copy, ts in zip((nc.vector.tensor_copy, nc.scalar.copy), PAIRS):
+            for copy, ts in zip((first, nc.scalar.copy), PAIRS):
                 deal(copy, dealt[:, ts, :, :], raw, ts)
             for t in range(PACK):
                 quantise(w2_codes[:, t, ms], w2_scales[:, t, ms], dealt[:, t, :, :].rearrange("p m j -> p (m j)"))

@@ -81,8 +81,9 @@ def tile_picked_phmix_sigmoid_po_kernel(
                     plane[QUAD * q : QUAD * q + 4, :].bitcast(I32),
                     picked[QUAD * q : QUAD * (q + 1) : BLOCK_P, :].bitcast(I32),
                 )
+            return picked
 
-        pick_bytes(offs_sb, heads_plane, "heads_bytes")
+        heads_bytes = pick_bytes(offs_sb, heads_plane, "heads_bytes")
         load_half(w2_raw[0], w2, 0, PAIRS[1])
         load_half(w2_raw[1], w2, 1, SLOTS)
         pick_bytes(own_sb, own_plane, "own_bytes")
@@ -90,6 +91,17 @@ def tile_picked_phmix_sigmoid_po_kernel(
         heads_words = keep.tile([P, S], U32, name="heads_words", align_bytes=64)
         own_words = keep.tile([P, S], U32, name="own_words", align_bytes=64)
         nc.vector.tensor_copy(heads_words[:], word_table[:].bitcast(U32).indirect(offs_sb[:]))
+        for bank in ("bank_5", "bank_6"):
+            idle = psum.tile([P, S], F32, name=bank, tag=bank)
+            nc.tensor.matmul_mx(
+                out=idle[:],
+                lhsT=heads_words[:, 0:P].bitcast(FP8X4),
+                lhsT_scale=heads_bytes[:, 0:P],
+                rhs=heads_words[:].bitcast(FP8X4),
+                rhs_scale=heads_bytes[:],
+                start=True,
+                stop=True,
+            )
         nc.vector.tensor_copy(own_words[:], word_table[:].bitcast(U32).indirect(own_sb[:]))
 
         def deal(copy, dealt, raw, ts):
@@ -129,20 +141,21 @@ def tile_picked_phmix_sigmoid_po_kernel(
 
         w1_mx, w2_mx = (w1_codes, w1_scales), (w2_codes, w2_scales)
 
-        def product(bank, weight, words, plane, h, ts):
+        def product(bank, weight, words, plane, h, ts, width=PLACES):
             codes, scales = weight
             acc = psum.tile([P, ts.stop - ts.start, PLACES], F32, name=bank, tag=bank)
-            cols = slice(h * PLACES, (h + 1) * PLACES)
             for t in range(ts.start, ts.stop):
-                nc.tensor.matmul_mx(
-                    out=acc[:, t - ts.start, :],
-                    lhsT=codes[:, t, :].bitcast(FP8X4),
-                    lhsT_scale=scales[:, t, :],
-                    rhs=words[:, cols].bitcast(FP8X4),
-                    rhs_scale=plane[:, cols],
-                    start=True,
-                    stop=True,
-                )
+                for c0 in range(0, PLACES, width):
+                    cols = slice(h * PLACES + c0, h * PLACES + c0 + width)
+                    nc.tensor.matmul_mx(
+                        out=acc[:, t - ts.start, c0 : c0 + width],
+                        lhsT=codes[:, t, :].bitcast(FP8X4),
+                        lhsT_scale=scales[:, t, :],
+                        rhs=words[:, cols].bitcast(FP8X4),
+                        rhs_scale=plane[:, cols],
+                        start=True,
+                        stop=True,
+                    )
             return acc
 
         gate = reuse.tile([P, 2, PACK, PLACES], F32, name="gate", offset=0, align_bytes=64)
@@ -157,8 +170,8 @@ def tile_picked_phmix_sigmoid_po_kernel(
             for slots, rows in steps(ts, min(step, ts.stop - ts.start)):
                 nc.scalar.activation(gate[:, h, slots, :], acc[:, rows, :], SIGMOID)
 
-        def gated(bank, h, ts, step=2):
-            acc = product(bank, w2_mx, own_words, own_plane, h, ts)
+        def gated(bank, h, ts, step=2, width=PLACES):
+            acc = product(bank, w2_mx, own_words, own_plane, h, ts, width)
             for slots, rows in steps(ts, min(step, ts.stop - ts.start)):
                 nc.vector.tensor_tensor(results[h][:, slots, :], acc[:, rows, :], gate[:, h, slots, :], MULT)
             nc.sync.dma_start(out_rows[:, ts, h * PLACES : (h + 1) * PLACES], results[h][:, ts, :])
@@ -171,8 +184,8 @@ def tile_picked_phmix_sigmoid_po_kernel(
         gated("bank_4", 0, slice(0, 1))
         gated("bank_5", 0, slice(1, 2))
         gated("bank_6", 0, PAIRS[1], 1)
-        gated("bank_0", 1, PAIRS[0], 1)
-        gated("bank_7", 1, PAIRS[1], 1)
+        gated("bank_0", 1, PAIRS[0], 1, P)
+        gated("bank_7", 1, PAIRS[1], 1, P)
 
         rounded = keep.tile([P, S, PACK], BF16, name="rounded", align_bytes=64)
 

@@ -21,9 +21,8 @@ PACK = 4
 QUAD = 32
 BLOCK_P = 8
 PAIRS = (slice(0, 2), slice(2, 4))
-HALVES = (slice(0, P // 2), slice(P // 2, P))
-SLOTS = slice(0, PACK)
 PLACES = S // 2
+HALF_M = P // 2
 SCALAR_PLACES = 96
 POOL_PLACES = 176
 FIRST = 512
@@ -41,7 +40,7 @@ def tile_picked_phmix_sigmoid_po_kernel(
 
         offs_sb = lists.tile([P, S // 16], U16, name="offs_sb")
         own_sb = lists.tile([P, S // 16], U16, name="own_sb")
-        byte_table = reuse.tile([P, T], U8, name="byte_table", offset=24576, align_bytes=64)
+        byte_table = keep.tile([P, T], U8, name="byte_table", align_bytes=64)
         nc.vector.memset(byte_table[:].bitcast(I32), 0)
         word_table = keep.tile([P, T], I32, name="word_table", align_bytes=64)
         word_rows = x_words[0].rearrange("p c r -> p (c r)").bitcast(I32)
@@ -51,141 +50,104 @@ def tile_picked_phmix_sigmoid_po_kernel(
         nc.sync.dma_start(byte_table[0:P:BLOCK_P, :].bitcast(I32), x_scales[0].bitcast(I32))
         nc.sync.dma_start(word_table[:, FIRST:T], word_rows[:, FIRST:T])
 
-        def raw_half(name, offset):
-            return reuse.tile([P, PACK, N // 2], F32, name=name, offset=offset, align_bytes=64)
-
-        def load_half(raw, w, half, js):
+        def load_half(raw, w, half):
             rows = w.rearrange("(p j) c -> p j c", j=PACK)
-            nc.sync.dma_start(raw[:, js, :], rows[:, js, half * N // 2 : (half + 1) * N // 2])
+            nc.sync.dma_start(raw[:], rows[:, :, half * N // 2 : (half + 1) * N // 2])
+            return raw
 
-        w1_raw = [raw_half(f"w1_raw_{i}", 16384 + 4096 * i) for i in range(2)]
-        w2_raw = [raw_half(f"w2_raw_{i}", 5120 - 4096 * i) for i in range(2)]
-        for half in range(2):
-            load_half(w1_raw[half], w1, half, SLOTS)
-        load_half(w2_raw[0], w2, 0, PAIRS[0])
+        raws = [keep.tile([P, PACK, N // 2], F32, name=f"raw_{i}", align_bytes=64) for i in range(3)]
+        raws.append(reuse.tile([P, PACK, N // 2], F32, name="raw_3", offset=7168, align_bytes=64))
+        for i, raw in enumerate(raws):
+            load_half(raw, (w1, w2)[i // 2], i % 2)
 
-        heads_plane = keep.tile([P, S], U8, name="heads_plane", align_bytes=64)
-        own_plane = keep.tile([P, S], U8, name="own_plane", align_bytes=64)
-        nc.vector.memset(heads_plane[:].bitcast(I32), 0)
-        nc.vector.memset(own_plane[:].bitcast(I32), 0)
+        planes = keep.tile([P, 2, S], U8, name="planes", align_bytes=64)
+        nc.vector.memset(planes[:].rearrange("p a c -> p (a c)").bitcast(I32), 0)
         warm = keep.tile([P, 8], F32, name="warm")
         nc.vector.memset(warm[:], 0.0)
         warm_out = keep.tile([P, 8], F32, name="warm_out")
         nc.scalar.activation(warm_out[:], warm[:], SIGMOID)
 
-        def pick_bytes(offsets, plane, name):
-            picked = keep.tile([P, S], U8, name=name, align_bytes=64)
-            nc.vector.tensor_copy(picked[:], byte_table[:].indirect(offsets[:]))
-            for q in range(P // QUAD):
-                nc.sync.dma_start(
-                    plane[QUAD * q : QUAD * q + 4, :].bitcast(I32),
-                    picked[QUAD * q : QUAD * (q + 1) : BLOCK_P, :].bitcast(I32),
-                )
-            return picked
-
-        heads_bytes = pick_bytes(offs_sb, heads_plane, "heads_bytes")
-        load_half(w2_raw[0], w2, 0, PAIRS[1])
-        load_half(w2_raw[1], w2, 1, SLOTS)
-        pick_bytes(own_sb, own_plane, "own_bytes")
+        picked = keep.tile([P, 2, S], U8, name="picked", align_bytes=64)
+        for a, offsets in enumerate((offs_sb, own_sb)):
+            nc.vector.tensor_copy(picked[:, a, :], byte_table[:].indirect(offsets[:]))
+        for q in range(P // QUAD):
+            nc.scalar.dma_start(
+                planes[QUAD * q : QUAD * q + 4, :, :].rearrange("p a c -> p (a c)").bitcast(I32),
+                picked[QUAD * q : QUAD * (q + 1) : BLOCK_P, :, :].rearrange("p a c -> p (a c)").bitcast(I32),
+            )
 
         heads_words = keep.tile([P, S], U32, name="heads_words", align_bytes=64)
-        own_words = keep.tile([P, S], U32, name="own_words", align_bytes=64)
         nc.vector.tensor_copy(heads_words[:], word_table[:].bitcast(U32).indirect(offs_sb[:]))
-        for bank in ("bank_5", "bank_6"):
-            idle = psum.tile([P, S], F32, name=bank, tag=bank)
+        own_words = [
+            keep.tile([P, PLACES], U32, name="own_words_0", align_bytes=64),
+            reuse.tile([P, PLACES], U32, name="own_words_1", offset=8192, align_bytes=64),
+        ]
+
+        def pick_own(h):
+            cols = slice(h * PLACES // 16, (h + 1) * PLACES // 16)
+            nc.vector.tensor_copy(own_words[h][:], word_table[:].bitcast(U32).indirect(own_sb[:, cols]))
+
+        pick_own(0)
+
+        codes = [keep.tile([P, PACK, P], U32, name=f"codes_{i}", align_bytes=64) for i in range(2)]
+        scales = [keep.tile([P, PACK, P], U8, name=f"scales_{i}", align_bytes=64) for i in range(2)]
+
+        def deal(copy, i, ts):
+            dealt = keep.tile([P, ts.stop - ts.start, HALF_M, PACK], BF16, name=f"dealt_{i}_{ts.start}", align_bytes=64)
+            copy(
+                dealt[:].rearrange("p t m j -> p m j t"),
+                raws[i][:].rearrange("p j (m t) -> p m j t", t=PACK)[:, :, :, ts],
+            )
+            return [dealt[:, t, :, :].rearrange("p m j -> p (m j)") for t in range(ts.stop - ts.start)]
+
+        def quantise(i, slots):
+            ms = slice(i % 2 * HALF_M, (i % 2 + 1) * HALF_M)
+            for t, dealt in enumerate(slots):
+                nc.vector.quantize_mx(out=codes[i // 2][:, t, ms].bitcast(FP8X4), scales=scales[i // 2][:, t, ms], in_=dealt)
+
+        def deal_shared(i):
+            return deal(nc.vector.tensor_copy, i, PAIRS[0]) + deal(nc.scalar.copy, i, PAIRS[1])
+
+        first = deal(nc.scalar.copy, 0, slice(0, PACK))
+        second = deal_shared(1)
+        quantise(0, first)
+        quantise(1, second)
+        for i in (2, 3):
+            quantise(i, deal_shared(i))
+        pick_own(1)
+
+        def product(acc, i, t, words, plane):
             nc.tensor.matmul_mx(
-                out=idle[:],
-                lhsT=heads_words[:, 0:P].bitcast(FP8X4),
-                lhsT_scale=heads_bytes[:, 0:P],
-                rhs=heads_words[:].bitcast(FP8X4),
-                rhs_scale=heads_bytes[:],
+                out=acc[:],
+                lhsT=codes[i][:, t, :].bitcast(FP8X4),
+                lhsT_scale=scales[i][:, t, :],
+                rhs=words.bitcast(FP8X4),
+                rhs_scale=plane,
                 start=True,
                 stop=True,
             )
-        nc.vector.tensor_copy(own_words[:], word_table[:].bitcast(U32).indirect(own_sb[:]))
-
-        def deal(copy, dealt, raw, ts):
-            copy(
-                dealt.rearrange("p t m j -> p m j t"),
-                raw[:].rearrange("p j (m t) -> p m j t", t=PACK)[:, :, :, ts],
-            )
-
-        def quantise(codes, scales, dealt):
-            nc.vector.quantize_mx(out=codes.bitcast(FP8X4), scales=scales, in_=dealt)
-
-        w1_codes = keep.tile([P, PACK, P], U32, name="w1_codes", align_bytes=64)
-        w1_scales = keep.tile([P, PACK, P], U8, name="w1_scales", align_bytes=64)
-        w2_codes = keep.tile([P, PACK, P], U32, name="w2_codes", align_bytes=64)
-        w2_scales = keep.tile([P, PACK, P], U8, name="w2_scales", align_bytes=64)
-
-        def quantise_weight(codes, scales, dealt):
-            for ts in PAIRS:
-                quantise(
-                    codes[:, ts, :].rearrange("p t m -> p (t m)"),
-                    scales[:, ts, :].rearrange("p t m -> p (t m)"),
-                    dealt[:, ts, :, :].rearrange("p t m j -> p (t m j)"),
-                )
-
-        w1_dealt = keep.tile([P, PACK, P, PACK], BF16, name="w1_dealt", align_bytes=64)
-        deal(nc.scalar.copy, w1_dealt[:, :, HALVES[0], :], w1_raw[0], SLOTS)
-        for ts in PAIRS:
-            deal(nc.scalar.copy, w1_dealt[:, ts, HALVES[1], :], w1_raw[1], ts)
-        quantise_weight(w1_codes, w1_scales, w1_dealt)
-
-        for half, (ms, raw, first) in enumerate(zip(HALVES, w2_raw, (nc.scalar.copy, nc.vector.tensor_copy))):
-            dealt = keep.tile([P, PACK, P // 2, PACK], BF16, name=f"w2_dealt_{half}", align_bytes=64)
-            for copy, ts in zip((first, nc.scalar.copy), PAIRS):
-                deal(copy, dealt[:, ts, :, :], raw, ts)
-            for t in range(PACK):
-                quantise(w2_codes[:, t, ms], w2_scales[:, t, ms], dealt[:, t, :, :].rearrange("p m j -> p (m j)"))
-
-        w1_mx, w2_mx = (w1_codes, w1_scales), (w2_codes, w2_scales)
-
-        def product(bank, weight, words, plane, h, ts, width=PLACES):
-            codes, scales = weight
-            acc = psum.tile([P, ts.stop - ts.start, PLACES], F32, name=bank, tag=bank)
-            for t in range(ts.start, ts.stop):
-                for c0 in range(0, PLACES, width):
-                    cols = slice(h * PLACES + c0, h * PLACES + c0 + width)
-                    nc.tensor.matmul_mx(
-                        out=acc[:, t - ts.start, c0 : c0 + width],
-                        lhsT=codes[:, t, :].bitcast(FP8X4),
-                        lhsT_scale=scales[:, t, :],
-                        rhs=words[:, cols].bitcast(FP8X4),
-                        rhs_scale=plane[:, cols],
-                        start=True,
-                        stop=True,
-                    )
-            return acc
 
         gate = reuse.tile([P, 2, PACK, PLACES], F32, name="gate", offset=0, align_bytes=64)
         results = [keep.tile([P, PACK, PLACES], F32, name=f"result_{h}", align_bytes=64) for h in range(2)]
         out_rows = out_0.rearrange("(p t) c -> p t c", t=PACK)
 
-        def steps(ts, step):
-            return [(slice(t, t + step), slice(t - ts.start, t - ts.start + step)) for t in range(ts.start, ts.stop, step)]
+        y = [psum.tile([P, S], F32, name=f"y_{t}") for t in range(PACK)]
+        for t in range(PACK):
+            product(y[t], 0, t, heads_words[:], planes[:, 0, :])
+        for h in range(2):
+            for t in range(PACK):
+                nc.scalar.activation(gate[:, h, t, :], y[t][:, h * PLACES : (h + 1) * PLACES], SIGMOID)
 
-        def heads(bank, h, ts, step=2):
-            acc = product(bank, w1_mx, heads_words, heads_plane, h, ts)
-            for slots, rows in steps(ts, min(step, ts.stop - ts.start)):
-                nc.scalar.activation(gate[:, h, slots, :], acc[:, rows, :], SIGMOID)
-
-        def gated(bank, h, ts, step=2, width=PLACES):
-            acc = product(bank, w2_mx, own_words, own_plane, h, ts, width)
-            for slots, rows in steps(ts, min(step, ts.stop - ts.start)):
-                nc.vector.tensor_tensor(results[h][:, slots, :], acc[:, rows, :], gate[:, h, slots, :], MULT)
-            nc.sync.dma_start(out_rows[:, ts, h * PLACES : (h + 1) * PLACES], results[h][:, ts, :])
-
-        heads("bank_0", 0, slice(0, 1))
-        heads("bank_7", 0, slice(1, 2))
-        heads("bank_1", 0, PAIRS[1], 1)
-        heads("bank_2", 1, PAIRS[0], 1)
-        heads("bank_3", 1, PAIRS[1], 1)
-        gated("bank_4", 0, slice(0, 1))
-        gated("bank_5", 0, slice(1, 2))
-        gated("bank_6", 0, PAIRS[1], 1)
-        gated("bank_0", 1, PAIRS[0], 1, P)
-        gated("bank_7", 1, PAIRS[1], 1, P)
+        for h in range(2):
+            cols = slice(h * PLACES, (h + 1) * PLACES)
+            for t in range(PACK):
+                e = psum.tile([P, PLACES], F32, name=f"e_{t}", tag=f"e_{t}")
+                product(e, 1, t, own_words[h][:], planes[:, 1, cols])
+                nc.vector.tensor_tensor(results[h][:, t, :], e[:], gate[:, h, t, :], MULT)
+                if h == 0 and t < 2:
+                    nc.sync.dma_start(out_rows[:, t, cols], results[h][:, t, :])
+                elif t % 2:
+                    nc.sync.dma_start(out_rows[:, t - 1 : t + 1, cols], results[h][:, t - 1 : t + 1, :])
 
         rounded = keep.tile([P, S, PACK], BF16, name="rounded", align_bytes=64)
 
@@ -195,28 +157,27 @@ def tile_picked_phmix_sigmoid_po_kernel(
                 results[h][:, :, c0:c1].rearrange("p t (c i) -> p c t i", i=4),
             )
 
-        def pool_copy(out, in_):
-            nc.gpsimd.tensor_scalar(out, in_, 1.0, -0.0, MULT, ADD)
-
-        pool_copy(rounded[:, 0:POOL_PLACES, :], results[0][:, :, 0:POOL_PLACES].rearrange("p t c -> p c t"))
+        nc.gpsimd.tensor_scalar(
+            rounded[:, 0:POOL_PLACES, :], results[0][:, :, 0:POOL_PLACES].rearrange("p t c -> p c t"), 1.0, -0.0, MULT, ADD
+        )
         interleave(nc.scalar.copy, 0, POOL_PLACES, PLACES)
         interleave(nc.scalar.copy, 1, 0, SCALAR_PLACES)
         interleave(nc.vector.tensor_copy, 1, SCALAR_PLACES, PLACES)
 
         out_words = out_1[0].rearrange("p c r -> p (c r)").bitcast(I32)
-        codes = reuse.tile([P, S], I32, name="codes", offset=6144, align_bytes=64)
-        scales = keep.tile([P, S], U8, name="scales", align_bytes=64)
+        out_codes = reuse.tile([P, S], I32, name="out_codes", offset=6144, align_bytes=64)
+        out_scales = keep.tile([P, S], U8, name="out_scales", align_bytes=64)
         for h in range(2):
             cols = slice(h * PLACES, (h + 1) * PLACES)
             nc.vector.quantize_mx(
-                out=codes[:, cols].bitcast(FP8X4),
-                scales=scales[:, cols],
+                out=out_codes[:, cols].bitcast(FP8X4),
+                scales=out_scales[:, cols],
                 in_=rounded[:, cols, :].rearrange("p c t -> p (c t)"),
             )
-            nc.sync.dma_start(out_words[:, cols], codes[:, cols])
+            nc.sync.dma_start(out_words[:, cols], out_codes[:, cols])
         for q in range(P // QUAD):
             queue = nc.scalar if q % 2 else nc.sync
             queue.dma_start(
                 out_2[0, 4 * q : 4 * q + 4, :].bitcast(I32),
-                scales[QUAD * q : QUAD * q + 4, :].bitcast(I32),
+                out_scales[QUAD * q : QUAD * q + 4, :].bitcast(I32),
             )

@@ -50,37 +50,44 @@ def tile_picked_phmix_sigmoid_po_kernel(
         nc.sync.dma_start(byte_table[0:P:BLOCK_P, :].bitcast(I32), x_scales[0].bitcast(I32))
         nc.sync.dma_start(word_table[:, FIRST:T], word_rows[:, FIRST:T])
 
-        def load_half(raw, w, half):
-            rows = w.rearrange("(p j) c -> p j c", j=PACK)
-            nc.sync.dma_start(raw[:], rows[:, :, half * N // 2 : (half + 1) * N // 2])
-            return raw
+        def load_half(i, js):
+            rows = (w1, w2)[i // 2].rearrange("(p j) c -> p j c", j=PACK)
+            nc.sync.dma_start(raws[i][:, js, :], rows[:, js, i % 2 * N // 2 : (i % 2 + 1) * N // 2])
 
-        raws = [keep.tile([P, PACK, N // 2], F32, name=f"raw_{i}", align_bytes=64) for i in range(3)]
-        raws.append(reuse.tile([P, PACK, N // 2], F32, name="raw_3", offset=7168, align_bytes=64))
-        for i, raw in enumerate(raws):
-            load_half(raw, (w1, w2)[i // 2], i % 2)
+        raws = [
+            reuse.tile([P, PACK, N // 2], F32, name=f"raw_{i}", offset=offset, align_bytes=64)
+            for i, offset in enumerate((20480, 16384, 12288, 7168))
+        ]
+        load_half(0, slice(0, PACK))
+        load_half(1, slice(0, PACK))
 
-        planes = keep.tile([P, 2, S], U8, name="planes", align_bytes=64)
-        nc.vector.memset(planes[:].rearrange("p a c -> p (a c)").bitcast(I32), 0)
+        planes = [keep.tile([P, S], U8, name=f"plane_{a}", align_bytes=64) for a in range(2)]
+        for plane in planes:
+            nc.vector.memset(plane[:].bitcast(I32), 0)
         warm = keep.tile([P, 8], F32, name="warm")
         nc.vector.memset(warm[:], 0.0)
         warm_out = keep.tile([P, 8], F32, name="warm_out")
         nc.scalar.activation(warm_out[:], warm[:], SIGMOID)
 
-        picked = keep.tile([P, 2, S], U8, name="picked", align_bytes=64)
-        for a, offsets in enumerate((offs_sb, own_sb)):
-            nc.vector.tensor_copy(picked[:, a, :], byte_table[:].indirect(offsets[:]))
-        for q in range(P // QUAD):
-            nc.scalar.dma_start(
-                planes[QUAD * q : QUAD * q + 4, :, :].rearrange("p a c -> p (a c)").bitcast(I32),
-                picked[QUAD * q : QUAD * (q + 1) : BLOCK_P, :, :].rearrange("p a c -> p (a c)").bitcast(I32),
-            )
+        def pick_bytes(a, offsets):
+            picked = keep.tile([P, S], U8, name=f"picked_{a}", align_bytes=64)
+            nc.vector.tensor_copy(picked[:], byte_table[:].indirect(offsets[:]))
+            for q in range(P // QUAD):
+                nc.sync.dma_start(
+                    planes[a][QUAD * q : QUAD * q + 4, :].bitcast(I32),
+                    picked[QUAD * q : QUAD * (q + 1) : BLOCK_P, :].bitcast(I32),
+                )
+
+        pick_bytes(0, offs_sb)
+        load_half(2, slice(0, PACK))
+        load_half(3, slice(0, PACK))
+        pick_bytes(1, own_sb)
 
         heads_words = keep.tile([P, S], U32, name="heads_words", align_bytes=64)
         nc.vector.tensor_copy(heads_words[:], word_table[:].bitcast(U32).indirect(offs_sb[:]))
         own_words = [
             keep.tile([P, PLACES], U32, name="own_words_0", align_bytes=64),
-            reuse.tile([P, PLACES], U32, name="own_words_1", offset=8192, align_bytes=64),
+            reuse.tile([P, PLACES], U32, name="own_words_1", offset=16384, align_bytes=64),
         ]
 
         def pick_own(h):
@@ -100,25 +107,28 @@ def tile_picked_phmix_sigmoid_po_kernel(
             )
             return [dealt[:, t, :, :].rearrange("p m j -> p (m j)") for t in range(ts.stop - ts.start)]
 
-        def quantise(i, slots):
+        def quantise(i, t, dealt):
             ms = slice(i % 2 * HALF_M, (i % 2 + 1) * HALF_M)
-            for t, dealt in enumerate(slots):
-                nc.vector.quantize_mx(out=codes[i // 2][:, t, ms].bitcast(FP8X4), scales=scales[i // 2][:, t, ms], in_=dealt)
+            nc.vector.quantize_mx(out=codes[i // 2][:, t, ms].bitcast(FP8X4), scales=scales[i // 2][:, t, ms], in_=dealt)
 
         def deal_shared(i):
             return deal(nc.vector.tensor_copy, i, PAIRS[0]) + deal(nc.scalar.copy, i, PAIRS[1])
 
         first = deal(nc.scalar.copy, 0, slice(0, PACK))
         second = deal_shared(1)
-        quantise(0, first)
-        quantise(1, second)
-        for i in (2, 3):
-            quantise(i, deal_shared(i))
+        for t in range(PACK):
+            quantise(0, t, first[t])
+            quantise(1, t, second[t])
         pick_own(1)
+        third = deal(nc.scalar.copy, 2, PAIRS[0]) + deal(nc.scalar.copy, 2, PAIRS[1])
+        fourth = deal_shared(3)
+        for t in range(PACK):
+            quantise(2, t, third[t])
+            quantise(3, t, fourth[t])
 
         def product(acc, i, t, words, plane):
             nc.tensor.matmul_mx(
-                out=acc[:],
+                out=acc,
                 lhsT=codes[i][:, t, :].bitcast(FP8X4),
                 lhsT_scale=scales[i][:, t, :],
                 rhs=words.bitcast(FP8X4),
@@ -131,23 +141,21 @@ def tile_picked_phmix_sigmoid_po_kernel(
         results = [keep.tile([P, PACK, PLACES], F32, name=f"result_{h}", align_bytes=64) for h in range(2)]
         out_rows = out_0.rearrange("(p t) c -> p t c", t=PACK)
 
-        y = [psum.tile([P, S], F32, name=f"y_{t}") for t in range(PACK)]
-        for t in range(PACK):
-            product(y[t], 0, t, heads_words[:], planes[:, 0, :])
-        for h in range(2):
-            for t in range(PACK):
-                nc.scalar.activation(gate[:, h, t, :], y[t][:, h * PLACES : (h + 1) * PLACES], SIGMOID)
+        units = ((0, slice(0, 1)), (0, slice(1, 2)), (0, PAIRS[1]), (1, PAIRS[0]), (1, PAIRS[1]))
 
-        for h in range(2):
-            cols = slice(h * PLACES, (h + 1) * PLACES)
-            for t in range(PACK):
-                e = psum.tile([P, PLACES], F32, name=f"e_{t}", tag=f"e_{t}")
-                product(e, 1, t, own_words[h][:], planes[:, 1, cols])
-                nc.vector.tensor_tensor(results[h][:, t, :], e[:], gate[:, h, t, :], MULT)
-                if h == 0 and t < 2:
-                    nc.sync.dma_start(out_rows[:, t, cols], results[h][:, t, :])
-                elif t % 2:
-                    nc.sync.dma_start(out_rows[:, t - 1 : t + 1, cols], results[h][:, t - 1 : t + 1, :])
+        def products(bank, i, h, ts, words, plane):
+            acc = psum.tile([P, ts.stop - ts.start, PLACES], F32, name=f"bank_{bank}", tag=f"bank_{bank}")
+            for t in range(ts.start, ts.stop):
+                product(acc[:, t - ts.start, :], i, t, words, plane[:, h * PLACES : (h + 1) * PLACES])
+            return [(t, acc[:, t - ts.start, :]) for t in range(ts.start, ts.stop)]
+
+        for bank, (h, ts) in enumerate(units):
+            for t, y in products(bank, 0, h, ts, heads_words[:, h * PLACES : (h + 1) * PLACES], planes[0]):
+                nc.scalar.activation(gate[:, h, t, :], y, SIGMOID)
+        for bank, (h, ts) in zip((5, 6, 7, 0, 1), units):
+            for t, e in products(bank, 1, h, ts, own_words[h][:], planes[1]):
+                nc.vector.tensor_tensor(results[h][:, t, :], e, gate[:, h, t, :], MULT)
+            nc.sync.dma_start(out_rows[:, ts, h * PLACES : (h + 1) * PLACES], results[h][:, ts, :])
 
         rounded = keep.tile([P, S, PACK], BF16, name="rounded", align_bytes=64)
 

@@ -60,6 +60,7 @@ def tile_picked_phmix_sigmoid_po_kernel(
         ]
         load_half(0, slice(0, PACK))
         load_half(1, slice(0, PACK))
+        load_half(2, PAIRS[0])
 
         planes = [keep.tile([P, S], U8, name=f"plane_{a}", align_bytes=64) for a in range(2)]
         for plane in planes:
@@ -79,7 +80,7 @@ def tile_picked_phmix_sigmoid_po_kernel(
                 )
 
         pick_bytes(0, offs_sb)
-        load_half(2, slice(0, PACK))
+        load_half(2, PAIRS[1])
         load_half(3, slice(0, PACK))
         pick_bytes(1, own_sb)
 

@@ -150,13 +150,21 @@ def tile_picked_phmix_sigmoid_po_kernel(
                 product(acc[:, t - ts.start, :], i, t, words, plane[:, h * PLACES : (h + 1) * PLACES])
             return [(t, acc[:, t - ts.start, :]) for t in range(ts.start, ts.stop)]
 
-        for bank, (h, ts) in enumerate(units):
+        def gates(bank, h, ts):
             for t, y in products(bank, 0, h, ts, heads_words[:, h * PLACES : (h + 1) * PLACES], planes[0]):
                 nc.scalar.activation(gate[:, h, t, :], y, SIGMOID)
-        for bank, (h, ts) in zip((5, 6, 7, 0, 1), units):
+
+        def gated(bank, h, ts):
             for t, e in products(bank, 1, h, ts, own_words[h][:], planes[1]):
                 nc.vector.tensor_tensor(results[h][:, t, :], e, gate[:, h, t, :], MULT)
             nc.sync.dma_start(out_rows[:, ts, h * PLACES : (h + 1) * PLACES], results[h][:, ts, :])
+
+        for bank, (h, ts) in enumerate(units[:4]):
+            gates(bank, h, ts)
+        for bank, (h, ts) in enumerate(units[:4], 4):
+            gated(bank, h, ts)
+        gates(4, *units[4])
+        gated(5, *units[4])
 
         rounded = keep.tile([P, S, PACK], BF16, name="rounded", align_bytes=64)
 

@@ -26,6 +26,7 @@ HALF_M = P // 2
 SCALAR_PLACES = 96
 POOL_PLACES = 176
 FIRST = 512
+AHEAD = 1
 
 
 def tile_picked_phmix_sigmoid_po_kernel(
@@ -60,7 +61,7 @@ def tile_picked_phmix_sigmoid_po_kernel(
         ]
         load_half(0, slice(0, PACK))
         load_half(1, slice(0, PACK))
-        load_half(2, PAIRS[0])
+        load_half(2, slice(0, AHEAD))
 
         planes = [keep.tile([P, S], U8, name=f"plane_{a}", align_bytes=64) for a in range(2)]
         for plane in planes:
@@ -80,7 +81,7 @@ def tile_picked_phmix_sigmoid_po_kernel(
                 )
 
         pick_bytes(0, offs_sb)
-        load_half(2, PAIRS[1])
+        load_half(2, slice(AHEAD, PACK))
         load_half(3, slice(0, PACK))
         pick_bytes(1, own_sb)
 
@@ -161,10 +162,11 @@ def tile_picked_phmix_sigmoid_po_kernel(
 
         for bank, (h, ts) in enumerate(units[:4]):
             gates(bank, h, ts)
-        for bank, (h, ts) in enumerate(units[:4], 4):
+        gates(7, 1, slice(2, 3))
+        for bank, (h, ts) in zip((4, 5, 6, 0), units[:4]):
             gated(bank, h, ts)
-        gates(4, *units[4])
-        gated(5, *units[4])
+        gates(4, 1, slice(3, 4))
+        gated(1, *units[4])
 
         rounded = keep.tile([P, S, PACK], BF16, name="rounded", align_bytes=64)
 

@@ -46,9 +46,9 @@ def tile_picked_phmix_sigmoid_po_kernel(
         word_table = keep.tile([P, T], I32, name="word_table", align_bytes=64)
         word_rows = x_words[0].rearrange("p c r -> p (c r)").bitcast(I32)
         nc.sync.dma_start(word_table[:, 0:FIRST], word_rows[:, 0:FIRST])
+        nc.sync.dma_start(byte_table[0:P:BLOCK_P, :].bitcast(I32), x_scales[0].bitcast(I32))
         nc.sync.dma_start(offs_sb[:], offs)
         nc.sync.dma_start(own_sb[:], own)
-        nc.sync.dma_start(byte_table[0:P:BLOCK_P, :].bitcast(I32), x_scales[0].bitcast(I32))
         nc.sync.dma_start(word_table[:, FIRST:T], word_rows[:, FIRST:T])
 
         def load_half(i, js):

from contextlib import ExitStack

import concourse.mybir as mybir

K, T, S, N = 512, 2048, 512, 512
FLOPS = 2 * 2 * K * N * S

F32 = mybir.dt.float32
BF16 = mybir.dt.bfloat16
I32 = mybir.dt.int32
U32 = mybir.dt.uint32
U16 = mybir.dt.uint16
U8 = mybir.dt.uint8
FP8X4 = mybir.dt.float8_e4m3fn_x4
SIGMOID = mybir.ActivationFunctionType.Sigmoid
MULT = mybir.AluOpType.mult
ADD = mybir.AluOpType.add

P = 128
PACK = 4
QUAD = 32
BLOCK_P = 8
PAIRS = (slice(0, 2), slice(2, 4))
PLACES = S // 2
HALF_M = P // 2
SCALAR_PLACES = 96
POOL_PLACES = 176
FIRST = 512
AHEAD = 1


def tile_picked_phmix_sigmoid_po_kernel(
    tc, x_words, x_scales, w1, w2, offs, own, out_0, out_1, out_2
):
    nc = tc.nc
    with ExitStack() as ctx:
        lists = ctx.enter_context(tc.tile_pool(name="lists", bufs=1))
        reuse = ctx.enter_context(tc.tile_pool(name="reuse", bufs=1))
        keep = ctx.enter_context(tc.tile_pool(name="keep", bufs=1))
        psum = ctx.enter_context(tc.psum_pool(name="psum", bufs=1))

        offs_sb = lists.tile([P, S // 16], U16, name="offs_sb")
        own_sb = lists.tile([P, S // 16], U16, name="own_sb")
        byte_table = keep.tile([P, T], U8, name="byte_table", align_bytes=64)
        nc.vector.memset(byte_table[:].bitcast(I32), 0)
        word_table = keep.tile([P, T], I32, name="word_table", align_bytes=64)
        word_rows = x_words[0].rearrange("p c r -> p (c r)").bitcast(I32)
        nc.sync.dma_start(word_table[:, 0:FIRST], word_rows[:, 0:FIRST])
        nc.sync.dma_start(byte_table[0:P:BLOCK_P, :].bitcast(I32), x_scales[0].bitcast(I32))
        nc.sync.dma_start(offs_sb[:], offs)
        nc.sync.dma_start(own_sb[:], own)
        nc.sync.dma_start(word_table[:, FIRST:T], word_rows[:, FIRST:T])

        def load_half(i, js):
            rows = (w1, w2)[i // 2].rearrange("(p j) c -> p j c", j=PACK)
            nc.sync.dma_start(raws[i][:, js, :], rows[:, js, i % 2 * N // 2 : (i % 2 + 1) * N // 2])

        raws = [
            reuse.tile([P, PACK, N // 2], F32, name=f"raw_{i}", offset=offset, align_bytes=64)
            for i, offset in enumerate((20480, 16384, 12288, 7168))
        ]
        load_half(0, slice(0, PACK))
        load_half(1, slice(0, PACK))
        load_half(2, slice(0, AHEAD))

        planes = [keep.tile([P, S], U8, name=f"plane_{a}", align_bytes=64) for a in range(2)]
        for plane in planes:
            nc.vector.memset(plane[:].bitcast(I32), 0)
        warm = keep.tile([P, 8], F32, name="warm")
        nc.vector.memset(warm[:], 0.0)
        warm_out = keep.tile([P, 8], F32, name="warm_out")
        nc.scalar.activation(warm_out[:], warm[:], SIGMOID)

        def pick_bytes(a, offsets):
            picked = keep.tile([P, S], U8, name=f"picked_{a}", align_bytes=64)
            nc.vector.tensor_copy(picked[:], byte_table[:].indirect(offsets[:]))
            for q in range(P // QUAD):
                nc.sync.dma_start(
                    planes[a][QUAD * q : QUAD * q + 4, :].bitcast(I32),
                    picked[QUAD * q : QUAD * (q + 1) : BLOCK_P, :].bitcast(I32),
                )

        pick_bytes(0, offs_sb)
        load_half(2, slice(AHEAD, PACK))
        load_half(3, slice(0, PACK))
        pick_bytes(1, own_sb)

        heads_words = keep.tile([P, S], U32, name="heads_words", align_bytes=64)
        nc.vector.tensor_copy(heads_words[:], word_table[:].bitcast(U32).indirect(offs_sb[:]))
        own_words = [
            keep.tile([P, PLACES], U32, name="own_words_0", align_bytes=64),
            reuse.tile([P, PLACES], U32, name="own_words_1", offset=16384, align_bytes=64),
        ]

        def pick_own(h):
            cols = slice(h * PLACES // 16, (h + 1) * PLACES // 16)
            nc.vector.tensor_copy(own_words[h][:], word_table[:].bitcast(U32).indirect(own_sb[:, cols]))

        pick_own(0)

        codes = [keep.tile([P, PACK, P], U32, name=f"codes_{i}", align_bytes=64) for i in range(2)]
        scales = [keep.tile([P, PACK, P], U8, name=f"scales_{i}", align_bytes=64) for i in range(2)]

        def deal(copy, i, ts):
            dealt = keep.tile([P, ts.stop - ts.start, HALF_M, PACK], BF16, name=f"dealt_{i}_{ts.start}", align_bytes=64)
            copy(
                dealt[:].rearrange("p t m j -> p m j t"),
                raws[i][:].rearrange("p j (m t) -> p m j t", t=PACK)[:, :, :, ts],
            )
            return [dealt[:, t, :, :].rearrange("p m j -> p (m j)") for t in range(ts.stop - ts.start)]

        def quantise(i, t, dealt):
            ms = slice(i % 2 * HALF_M, (i % 2 + 1) * HALF_M)
            nc.vector.quantize_mx(out=codes[i // 2][:, t, ms].bitcast(FP8X4), scales=scales[i // 2][:, t, ms], in_=dealt)

        def deal_shared(i):
            return deal(nc.vector.tensor_copy, i, PAIRS[0]) + deal(nc.scalar.copy, i, PAIRS[1])

        first = deal(nc.scalar.copy, 0, slice(0, PACK))
        second = deal_shared(1)
        for t in range(PACK):
            quantise(0, t, first[t])
            quantise(1, t, second[t])
        pick_own(1)
        third = deal(nc.scalar.copy, 2, PAIRS[0]) + deal(nc.scalar.copy, 2, PAIRS[1])
        fourth = deal_shared(3)
        for t in range(PACK):
            quantise(2, t, third[t])
            quantise(3, t, fourth[t])

        def product(acc, i, t, words, plane):
            nc.tensor.matmul_mx(
                out=acc,
                lhsT=codes[i][:, t, :].bitcast(FP8X4),
                lhsT_scale=scales[i][:, t, :],
                rhs=words.bitcast(FP8X4),
                rhs_scale=plane,
                start=True,
                stop=True,
            )

        gate = reuse.tile([P, 2, PACK, PLACES], F32, name="gate", offset=0, align_bytes=64)
        results = [keep.tile([P, PACK, PLACES], F32, name=f"result_{h}", align_bytes=64) for h in range(2)]
        out_rows = out_0.rearrange("(p t) c -> p t c", t=PACK)

        units = ((0, slice(0, 1)), (0, slice(1, 2)), (0, PAIRS[1]), (1, PAIRS[0]), (1, PAIRS[1]))

        def products(bank, i, h, ts, words, plane):
            acc = psum.tile([P, ts.stop - ts.start, PLACES], F32, name=f"bank_{bank}", tag=f"bank_{bank}")
            for t in range(ts.start, ts.stop):
                product(acc[:, t - ts.start, :], i, t, words, plane[:, h * PLACES : (h + 1) * PLACES])
            return [(t, acc[:, t - ts.start, :]) for t in range(ts.start, ts.stop)]

        def gates(bank, h, ts):
            for t, y in products(bank, 0, h, ts, heads_words[:, h * PLACES : (h + 1) * PLACES], planes[0]):
                nc.scalar.activation(gate[:, h, t, :], y, SIGMOID)

        def gated(bank, h, ts):
            for t, e in products(bank, 1, h, ts, own_words[h][:], planes[1]):
                nc.vector.tensor_tensor(results[h][:, t, :], e, gate[:, h, t, :], MULT)
            nc.sync.dma_start(out_rows[:, ts, h * PLACES : (h + 1) * PLACES], results[h][:, ts, :])

        for bank, (h, ts) in enumerate(units[:4]):
            gates(bank, h, ts)
        gates(7, 1, slice(2, 3))
        for bank, (h, ts) in zip((4, 5, 6, 0), units[:4]):
            gated(bank, h, ts)
        gates(4, 1, slice(3, 4))
        gated(1, *units[4])

        rounded = keep.tile([P, S, PACK], BF16, name="rounded", align_bytes=64)

        def interleave(copy, h, c0, c1):
            copy(
                rounded[:, h * PLACES + c0 : h * PLACES + c1, :].rearrange("p (c i) t -> p c t i", i=4),
                results[h][:, :, c0:c1].rearrange("p t (c i) -> p c t i", i=4),
            )

        nc.gpsimd.tensor_scalar(
            rounded[:, 0:POOL_PLACES, :], results[0][:, :, 0:POOL_PLACES].rearrange("p t c -> p c t"), 1.0, -0.0, MULT, ADD
        )
        interleave(nc.scalar.copy, 0, POOL_PLACES, PLACES)
        interleave(nc.scalar.copy, 1, 0, SCALAR_PLACES)
        interleave(nc.vector.tensor_copy, 1, SCALAR_PLACES, PLACES)

        out_words = out_1[0].rearrange("p c r -> p (c r)").bitcast(I32)
        out_codes = reuse.tile([P, S], I32, name="out_codes", offset=6144, align_bytes=64)
        out_scales = keep.tile([P, S], U8, name="out_scales", align_bytes=64)
        for h in range(2):
            cols = slice(h * PLACES, (h + 1) * PLACES)
            nc.vector.quantize_mx(
                out=out_codes[:, cols].bitcast(FP8X4),
                scales=out_scales[:, cols],
                in_=rounded[:, cols, :].rearrange("p c t -> p (c t)"),
            )
            nc.sync.dma_start(out_words[:, cols], out_codes[:, cols])
        for q in range(P // QUAD):
            queue = nc.scalar if q % 2 else nc.sync
            queue.dma_start(
                out_2[0, 4 * q : 4 * q + 4, :].bitcast(I32),
                out_scales[QUAD * q : QUAD * q + 4, :].bitcast(I32),
            )
